import numpy as np, ml_dtypes
CORES = [16,17,18,19,150,151]
N = 6
BF = ml_dtypes.bfloat16
def gentries(a):
    return np.ascontiguousarray(a.reshape(8, 16, -1).transpose(0, 2, 1)).reshape(8, -1)
def gtable(e):
    e = np.asarray(e); return np.ascontiguousarray(e.reshape(8, -1, 16).transpose(0, 2, 1)).reshape(128, -1).astype(np.int32)
W, NB, T, CA, LV, LI, LG = 4096, 4096, 4, 5, 7, 2, 1
P, S = NB // 16, W // (NB // 16)
def parts(rng):
    return rng.integers(0, 256, (N, 8, 16, W)), rng.integers(0, 256, (N, 8, 16, P)), rng.integers(0, 16, (N, 8, 16)), rng.integers(0, W, (N, 8, NB)), rng.integers(0, W, (N, 8, NB))
def pack(x, z, w, a, b):
    return {"xt": np.reshape(x, (N, 128, W)).astype(np.float32).astype(BF), "zp": np.reshape(z, (N, 128, P)).astype(np.float32).astype(BF), "wl": np.reshape(w, (N, 128, 1)).astype(np.float32).astype(BF),
            "ba": np.stack([gtable(v) for v in a]), "bb": np.stack([gtable(v) for v in b])}
def setup_inputs(rng):
    x, z, w, a, b = parts(rng)
    return pack(x, z, w, a, np.where(rng.random(b.shape) < 0.125, a, b))
def setup_inputs_corners(rng):
    x, z, w, a, b = parts(rng); pol = 255 * (np.arange(8) & 1)
    good = rng.random((N, 8, W)) < 0.5; good[..., W - 4:W - 1] = False
    far = np.abs(pol[None, :, None, None] - rng.integers(128, 256, x.shape))
    x = np.where(good[:, :, None, :], pol[None, :, None, None], far)
    z = np.broadcast_to(pol[None, :, None, None], z.shape).copy()
    o = np.argsort(rng.random((N, 8, 16)), axis=-1); v = rng.choice(np.array([128, 200]), (N, 8, 16))
    x[..., W - 4] = 128; x[..., W - 3] = np.where(o < LV, v, 60); x[..., W - 2] = np.where(o < LV - 1, v, 60)
    own = np.arange(NB).reshape(P, 16)
    for q in range(N):
        for g in range(8):
            pa, pb = rng.integers(0, W, 8192), rng.integers(0, W, 8192); pc = ((pa * pb >> 5) + pa + 37 * pb) & (W - 1); k = good[q, g]
            yes = np.flatnonzero(~k[pa] & ~k[pb] & k[pc] & (pa != pb)); no = np.flatnonzero((k[pa] | k[pb]) & (pa != pb))
            n = rng.choice(np.array([0, 1, CA - 1, CA, CA + 1, 16]), P); n[P - 1] = CA; n[0] = 16; n[2] = CA + 1
            m = np.argsort(rng.random((P, 16)), axis=1) < n[:, None]
            i = np.where(m, yes[rng.integers(0, len(yes), (P, 16))], no[rng.integers(0, len(no), (P, 16))]); aa, bb = pa[i], pb[i]
            kp = rng.integers(0, 12, P); kp[0] = 9; kp[P - 1] = 9; kp[2] = 9; kp[1] = 2; kp[P - 2] = 3; kp[3] = 0; kp[P - 3] = 1
            s = (kp == 0) | (kp == 2) | (kp == 3); aa[s] = own[s]; bb[s] = own[s]
            e = (W - 1) * rng.integers(0, 2, (P, 16)); aa[kp == 1] = e[kp == 1]; bb[kp == 1] = e[kp == 1]
            aa[kp == 4] = e[kp == 4]; bb[kp == 4] = W - 1 - e[kp == 4]
            slot = rng.integers(0, 16, P)
            for c, col in ((2, W - 3), (3, W - 2)):
                r = np.flatnonzero(kp == c); aa[r, slot[r]] = W - 4; bb[r, slot[r]] = col; z[q, g][:, r] = x[q, g, :, col][:, None]
            a[q, g] = aa.reshape(-1); b[q, g] = bb.reshape(-1)
    b[1] = a[1]
    w[:, 0] = 0; w[:, 1] = 15; w[:, 2] = 0; w[:, 2, 15] = 15; w[:, 3] = 15 * rng.integers(0, 2, (N, 16))
    return pack(x, z, w, a, b)
def setup_inputs_ends(rng):
    kind = rng.integers(0, 4, (N, 8, 1, W)); x = 255 * np.where(kind > 1, rng.integers(0, 2, (N, 8, 16, W)), kind)
    x = np.where((kind == 3) & (rng.random(x.shape) < 0.25), x ^ 1, x)
    hi = np.arange(8) & 1
    x[..., 0] = 255 * (1 - hi)[None, :, None]; x[..., W - 1] = 255 * hi[None, :, None]; x[0, ::2, :, W - 37] = 255
    cc = (((W - 1) * (W - 2) >> 5) + W - 1 + 37 * (W - 2)) & (W - 1)
    x[:, 1::2, :, W - 2] = 255; x[:, 1::2, :, cc] = 255
    zk = rng.integers(0, 3, (N, 8, 1, P)); z = 255 * np.where(zk == 2, rng.integers(0, 2, (N, 8, 16, P)), zk)
    w = 15 * rng.integers(0, 2, (N, 8, 16)); w[:, 1] = 15; w[:, 7] = 15; w[:, 2] = 0
    sh = (N, 8, NB)
    a = np.where(rng.random(sh) < 0.8, (W - 1) * rng.integers(0, 2, sh), rng.integers(0, W, sh))
    b = np.where(rng.random(sh) < 0.8, (W - 1) * rng.integers(0, 2, sh), rng.integers(0, W, sh))
    n = rng.integers(10, 17, (8, P, 1)); n[:, 0] = 16; n[:, P - 1] = 16
    m = (np.argsort(rng.random((8, P, 16)), axis=-1) < n).reshape(8, NB); top = ((W - 1) * hi)[:, None]
    a[0] = np.where(m, top, a[0]); b[0] = np.where(m, W - 1 - top, b[0])
    z[0] = 255 * (np.argsort(rng.random((8, 16, P)), axis=1) < rng.integers(0, 7, (8, 1, P)))
    for q in range(1, N):
        for g in (1, 7):
            for i, va, vb, vz in ((0, 0, W - 1, 255), (P - 1, 0, W - 1, 255), (1, W - 1, 0, 0), (P - 2, W - 1, 0, 0), (2, W - 1, W - 2, 0), (P - 3, W - 1, W - 2, 0)):
                a[q, g, 16 * i:16 * i + 16] = va; b[q, g, 16 * i:16 * i + 16] = vb; z[q, g, :, i] = vz
    return pack(x, z, w, a, b)
def setup_inputs_spread(rng):
    x, z, w, a, b = parts(rng)
    x = (np.exp2(8 * rng.random((N, 8, 1, W))) * rng.random(x.shape)).astype(np.int64)
    z = (np.exp2(8 * rng.random((N, 8, 1, P))) * rng.random(z.shape)).astype(np.int64)
    w = w >> rng.integers(0, 5, w.shape)
    a = (W * rng.random(a.shape) ** rng.integers(1, 5, (N, 8, 1))).astype(np.int64); b = (W * rng.random(b.shape) ** rng.integers(1, 5, (N, 8, 1))).astype(np.int64)
    return pack(x, z, w, np.minimum(a, W - 1), np.minimum(b, W - 1))
def setup_inputs_ties(rng):
    x, z, w, a, b = parts(rng)
    base = rng.integers(0, 256, (N, 8, 16, 6)); base[:, ::2] = rng.choice(np.array([0, 1, 128, 254, 255]), (N, 4, 16, 6))
    x = np.take_along_axis(base, rng.integers(0, 6, (N, 8, 1, W)), 3)
    z = np.where(rng.random((N, 8, 1, P)) < 0.75, np.take_along_axis(base, rng.integers(0, 6, (N, 8, 1, P)), 3), z)
    m = rng.random((N, 8, P, 1)) < 0.25
    a = a.reshape(N, 8, P, 16); b = b.reshape(N, 8, P, 16); b = np.where(rng.random(b.shape) < 0.125, a, b)
    a = np.where(m, a[..., :1], a).reshape(N, 8, NB); b = np.where(m, b[..., :1], b).reshape(N, 8, NB)
    return pack(x, z, w, a, b)
def check_inputs(d):
    bad = []
    for k, lo, hi in (("xt", 0, 255), ("zp", 0, 255), ("wl", 0, 15), ("ba", 0, W - 1), ("bb", 0, W - 1)):
        v = np.asarray(d[k]).astype(np.float64)
        if not np.all((v >= lo) & (v <= hi) & (v == np.floor(v))): bad.append("range of " + k)
    return bad
def reference(xt, zp, wl, ba, bb):
    X = xt.astype(np.float32).astype(np.int32).reshape(N, 8, 16, W); z = zp.astype(np.float32).astype(np.int32).reshape(N, 8, 16, P)
    w = wl.astype(np.float32).astype(np.int32).reshape(N, 8, 16, 1)
    L = [np.stack([gentries(v) for v in m]).astype(np.int32) for m in (ba, bb)]
    I = np.zeros((N, 8, NB), np.int32); G = np.zeros((N, 8, NB), np.int32); rej = [0] * N
    def before(m):
        m = m.astype(np.int32).reshape(8, P, 16)
        return (np.add.accumulate(m, axis=2) - m).reshape(8, NB)
    for t in range(T):
        now = [0] * N
        for q in range(N):
            s = (q + t) % N
            H = L[t % 2][q]; O = L[1 - t % 2][q]; C = ((H * O >> 5) + H + 37 * O) & (W - 1)
            h, o, c = [np.take_along_axis(X[s], v[:, None, :], 2) for v in (H, O, C)]
            zz = np.repeat(z[q], 16, axis=2); dh, do, dc = [np.add.reduce(np.abs(v - zz), axis=1) for v in (h, o, c)]
            live = H != O
            rec = live & (do <= np.minimum(dh, dc))
            want = live & ~rec & (dc < dh) & (G[q] < LG); am = want & (before(want) < CA)
            ins = live & ~rec & ~am
            ch = np.where(rec[:, None, :], o, np.where(am[:, None, :], c, h))
            V = np.add.reduce((ch - h).reshape(8, 16, P, 16), axis=3)
            ok = np.add.reduce((V >= 0).astype(np.int32), axis=1) >= LV
            now[s] = int(np.add.reduce((~ok).astype(np.int64), axis=None)); yes = np.repeat(ok, 16, axis=1)
            I[q] += ins | ((rec | am) & ~yes); G[q] += am & yes
            H2 = np.where(yes & rec, O, np.where(yes & am, C, H))
            sp = I[q] >= LI; v = np.where((before(sp) & 1) == 1, C, H)
            H2 = np.where(sp, v, H2); O2 = np.where(sp, v, O); I[q] = np.where(sp, 0, I[q])
            M = np.maximum.reduce(ch.reshape(8, 16, P, 16), axis=3); u = np.add.reduce(w[s] * M, axis=1) & (W - 1)
            O2 = np.where(live, O2, ((H * np.repeat(u, 16, axis=1) >> 5) + H + rej[s]) & (W - 1))
            L[t % 2][q] = H2; L[1 - t % 2][q] = O2
            if t < T - 1:
                z[q] = np.abs(z[q] - M)
                at = (S * np.arange(P)[None, :] + (u & (S - 1)))[:, None, :]
                np.put_along_axis(X[s], at, (np.take_along_axis(X[s], at, 2) + M) >> 1, 2)
        rej = now
    home = [(s - (T - 1)) % N for s in range(N)]
    ya, yb, yi, yg = [np.stack([gtable(m[q]) for q in home]).astype(np.float32) for m in (L[0], L[1], I, G)]
    return {"ya": ya, "yb": yb, "yi": yi, "yg": yg}

@@ -1,0 +1,613 @@
+from concourse.mybir import dt, AluOpType as ALU, ActivationFunctionType as ACT
+
+CH = [96, 96, 64]
+NCH = len(CH)
+OFF = [sum(CH[:j]) for j in range(NCH)]
+NM = max(CH)
+NB = 3
+READS = 4
+NENG = 8
+PH, PD, PC, DHV = 48, 96, 96, False
+
+SCRATCH = {
+    "X": ("sbuf", [128, 4096], "bfloat16"),
+    "li": ("sbuf", [128, 512], "int32"),
+    "wcol": ("sbuf", [128, 1], "bfloat16"),
+    "Eb": ("sbuf", [128, 144], "bfloat16"), "Ew": ("sbuf", [128, 144], "bfloat16"),
+    "GBb": ("sbuf", [128, 128], "bfloat16"), "Ib": ("sbuf", [128, 128], "bfloat16"),
+    "Ibn": ("sbuf", [128, 128], "bfloat16"), "Ib128": ("sbuf", [128, 128], "bfloat16"),
+    "Ibh": ("sbuf", [128, 128], "bfloat16"), "TrS": ("sbuf", [128, 128], "bfloat16"),
+    "Tr1": ("sbuf", [128, 128], "bfloat16"), "ones": ("sbuf", [128, 144], "bfloat16"),
+    "tmpw": ("sbuf", [128, 144], "bfloat16"), "tmpw2": ("sbuf", [128, 144], "bfloat16"),
+    "tmpt": ("sbuf", [128, 128], "bfloat16"),
+    "H1": ("sbuf", [128, 128], "float16"), "Hn": ("sbuf", [128, 128], "float16"),
+    "H65": ("sbuf", [128, 128], "float16"), "H101": ("sbuf", [128, 128], "float16"),
+    "H2048": ("sbuf", [128, 128], "float16"), "H256": ("sbuf", [128, 128], "float16"),
+    "HK": ("sbuf", [128, 128], "float16"), "on16": ("sbuf", [128, NM], "float16"),
+    "F1": ("sbuf", [128, 128], "float32"), "FK": ("sbuf", [128, 128], "float32"),
+    "Wb": ("sbuf", [128, 128], "bfloat16"),
+    "bi": ("sbuf", [128, 32], "int32"), "base": ("sbuf", [128, 16], "int32"),
+    "RST": ("sbuf", [128, 16 * NM], "bfloat16"),
+    "kacc": ("sbuf", [128, 16], "float32"), "kcol": ("sbuf", [128, 1], "float32"),
+    "junk": ("sbuf", [128, NM], "bfloat16"),
+    "ul": ("sbuf", [128, 32], "int32"),
+    "nl": ("sbuf", [128, 32], "uint16"), "xv": ("sbuf", [128, 256], "int32"),
+    "oya": ("sbuf", [128, 256], "float32"), "oyb": ("sbuf", [128, 256], "float32"),
+    "oyi": ("sbuf", [128, 256], "float32"), "oyg": ("sbuf", [128, 256], "float32"),
+}
+for _t in range(READS):
+    SCRATCH["lu%d" % _t] = ("sbuf", [128, 512], "uint16")
+    SCRATCH["mz%d" % _t] = ("sbuf", [128, 768], "bfloat16")
+    if _t < READS - 1:
+        SCRATCH["su%d" % _t] = ("sbuf", [128, 512], "uint16")
+        SCRATCH["sz%d" % _t] = ("sbuf", [128, 768], "bfloat16")
+for _p in range(2):
+    SCRATCH["zs%d" % _p] = ("sbuf", [128, 16 * NM], "bfloat16")
+for _p in range(NB):
+    for _n in ("zr", "h", "do", "dc", "ah", "ao", "ac", "ch", "rm"):
+        SCRATCH["%s%d" % (_n, _p)] = ("sbuf", [128, 16 * NM], "bfloat16")
+    SCRATCH["f%d" % _p] = ("sbuf", [128, 8 * NM], "float32")
+    SCRATCH["b%d" % _p] = ("sbuf", [128, 9 * NM], "bfloat16")
+    SCRATCH["s%d" % _p] = ("sbuf", [128, 4 * NM], "float16")
+    SCRATCH["i%d" % _p] = ("sbuf", [128, 3 * NM], "int32")
+    SCRATCH["u%d" % _p] = ("sbuf", [128, 2 * NM], "uint16")
+for _p in range(8):
+    SCRATCH["p%d" % _p] = ("psum", [128, 512], "float32")
+
+SEMAPHORES = ["qv", "qt", "qa", "qg", "left"]
+SEMAPHORES += ["x%d" % k for k in range(4)] + ["la%d" % k for k in range(NCH)] + ["lz", "lw"]
+SEMAPHORES += ["rl%d_%d" % (t, j) for t in range(1, READS) for j in range(NCH)]
+SEMAPHORES += ["rz%d_%d" % (t, j) for t in range(1, READS) for j in range(NCH)]
+SEMAPHORES += ["out%d" % k for k in range(4 * NCH)]
+
+EST = {"cy": 1.0, "gam": 1.56, "scat": 3.0, "pec": 0.5, "fv": 10.0, "fa": 10.0, "ft": 5.0, "wake": 60.0, "net": 3500.0, "dma": 2000.0, "iss": 500.0}
+BONUS = {}
+
+
+def price(w, E):
+    k, n = w[0], w[1]
+    if k == "v":
+        return E["fv"] + E["cy"] * max(64.0, n)
+    if k == "vg":
+        return 50.0 + E["cy"] * E["gam"] * n
+    if k == "vs":
+        return 50.0 + E["cy"] * E["scat"] * n
+    if k == "a":
+        return E["fa"] + E["cy"] * n
+    if k == "ag":
+        return 65.0 + E["cy"] * E["gam"] * n
+    if k == "t":
+        return E["pec"] * n + E["ft"] * w[2]
+    return E[k] if k in E else n
+
+
+def cv(n, f=1.0):
+    return ("v", n * f)
+
+
+def ca(n, f=1.0):
+    return ("a", n) if f == 1.0 else ("ag", n)
+
+
+def schedule(ops, E, bonus):
+    N = len(ops)
+    W = E["wake"]
+    cost = [price(o["w"], E) for o in ops]
+    succ = [[] for _ in range(N)]
+    for k in range(N):
+        for d in ops[k]["deps"]:
+            succ[d].append(k)
+    bot = [0.0] * N
+    for k in range(N - 1, -1, -1):
+        bot[k] = cost[k] + W + max([bot[s] for s in succ[k]] + [0.0])
+    pri = [bot[k] + bonus.get(ops[k]["tag"], 0.0) for k in range(N)]
+    left = [len(o["deps"]) for o in ops]
+    ready, free, order = {}, {}, []
+    rt, fin = [0.0] * N, [0.0] * N
+    for k in range(N):
+        ready.setdefault(ops[k]["q"], [])
+        if left[k] == 0:
+            ready[ops[k]["q"]].append(k)
+    while len(order) < N:
+        best = None
+        for q, lst in ready.items():
+            if not lst:
+                continue
+            f = 0.0 if q == "n" else free.get(q, 0.0)
+            st = max(f, min([rt[k] for k in lst]))
+            if best is None or st < best[0]:
+                best = (st, q, lst)
+        st, q, lst = best
+        k = max([k for k in lst if rt[k] <= st + 1e-9], key=lambda k: pri[k])
+        lst.remove(k)
+        dma = q in ("s", "s2")
+        free[q] = st + (60.0 if dma else cost[k])
+        fin[k] = st + cost[k]
+        order.append(k)
+        for s in succ[k]:
+            left[s] -= 1
+            rt[s] = max(rt[s], fin[k] + W)
+            if left[s] == 0:
+                ready[ops[s]["q"]].append(s)
+    return order, fin
+
+
+def rank_program(g, core, T, topo):
+    rank = T.rank_of(core)
+    if rank is None:
+        return
+    ops = []
+    hist = {}
+    cur = ["c", 0]
+
+    def phase(name, j):
+        cur[0], cur[1] = "%s%d" % (name, j), 0
+
+    def R(name, a, b):
+        return (name, a, b)
+
+    def add(q, fn, rd, wr, cost, sem=None, inc=1, after=()):
+        k = len(ops)
+        deps = {}
+        for isw, regs in ((False, rd), (True, wr)):
+            for (nm, a, b) in regs:
+                bank = nm[0] == "p" and nm[1:].isdigit()
+                for (d, da, db, dw) in hist.get(nm, ()):
+                    same = ops[d]["q"] == q
+                    over = a < db and da < b
+                    if bank and not same:
+                        deps[d] = True
+                    elif over and (isw or dw):
+                        deps[d] = deps.get(d, False) or dw or not same
+        for d in after:
+            deps[d] = True
+        for isw, regs in ((False, rd), (True, wr)):
+            for (nm, a, b) in regs:
+                lst = hist.setdefault(nm, [])
+                if isw:
+                    bank = nm[0] == "p" and nm[1:].isdigit()
+                    if not bank:
+                        lst = [e for e in lst if not (a <= e[1] and e[2] <= b)]
+                    else:
+                        lst = lst[-24:]
+                    hist[nm] = lst
+                lst.append((k, a, b, isw))
+        deps.pop(k, None)
+        w = ("dma", 0) if q in ("s", "s2") else cost if isinstance(cost, tuple) else ("x", cost)
+        ops.append({"q": q, "fn": fn, "deps": deps, "w": w, "sem": sem, "inc": inc, "tag": "%s:%d" % (cur[0], cur[1])})
+        cur[1] += 1
+        return k
+
+    def V(name, a, b, step=1):
+        return (name, a, b, step)
+
+    def ap(v):
+        if len(v) == 5:
+            o = v[4]
+            return T[v[0]][:, v[1]:v[2]].indirect(T[o[0]][:, o[1]:o[2]])
+        if v[3] == 1:
+            return T[v[0]][:, v[1]:v[2]]
+        return T[v[0]][:, v[1]:v[2]:v[3]]
+
+    def ind(win, off):
+        return (win[0], win[1], win[2], 1, off)
+
+    def regs(*vs):
+        r = []
+        for v in vs:
+            r.append((v[0], v[1], v[2]))
+            if len(v) == 5:
+                r.append((v[4][0], v[4][1], v[4][2]))
+        return r
+
+    def cnt(v):
+        if len(v) == 5:
+            return 16 * (v[4][2] - v[4][1])
+        return (v[2] - v[1] + v[3] - 1) // v[3]
+
+    two = ("bfloat16", "uint16", "float16")
+
+    def half(*vs):
+        return 0.5 if all(SCRATCH[v[0]][2] in two for v in vs) else 1.0
+
+    def tt(out, in0, in1, op):
+        n = cnt(out) if len(out) < 5 else cnt(in0)
+        if len(in0) == 5:
+            c = ("vg", n)
+        else:
+            c = cv(n, 1.0 if (in0[0][0] == "p" or in1[0][0] == "p") else 2.0)
+        return add("v", lambda: g.vector.tensor_tensor(ap(out), ap(in0), ap(in1), op), regs(in0, in1), regs(out), c)
+
+    def ts(out, in0, s1, op0, s2=None, op1=None):
+        rd = regs(in0) + [(s[0], s[1], s[2]) for s in (s1, s2) if isinstance(s, tuple)]
+
+        def emit():
+            a1 = ap(s1) if isinstance(s1, tuple) else s1
+            a2 = ap(s2) if isinstance(s2, tuple) else s2
+            if op1 is None:
+                return g.vector.tensor_scalar(ap(out), ap(in0), a1, None, op0)
+            return g.vector.tensor_scalar(ap(out), ap(in0), a1, a2, op0, op1)
+        return add("v", emit, rd, regs(out), cv(cnt(in0), half(out, in0)))
+
+    def cp(out, in_):
+        if len(out) == 5:
+            c = ("vs", cnt(in_))
+            return add("v", lambda: g.vector.tensor_copy(ap(out), ap(in_)), regs(in_) + [(out[4][0], out[4][1], out[4][2])], [(out[0], out[1], out[2])], c)
+        return add("v", lambda: g.vector.tensor_copy(ap(out), ap(in_)), regs(in_), regs(out), cv(cnt(in_), half(out, in_)))
+
+    def scan(out, d0, d1, o0, o1):
+        return add("v", lambda: g.vector.tensor_tensor_scan(ap(out), ap(d0), ap(d1), 0.0, o0, o1), regs(d0, d1), regs(out), cv(cnt(out), 0.5))
+
+    def fill(out, c):
+        return add("v", lambda: g.vector.memset(ap(out), c), [], regs(out), cv(cnt(out), half(out)))
+
+    def act(out, in_, func, bias=0.0, scale=1.0, acc=None):
+        n = cnt(out)
+        c = ca(n, 2.0 if len(in_) == 5 else 1.0)
+        wr = regs(out) + (regs(acc) if acc is not None else [])
+
+        def emit():
+            if acc is not None:
+                return g.scalar.activation(ap(out), ap(in_), func, bias=bias, scale=scale, accum_out=ap(acc))
+            return g.scalar.activation(ap(out), ap(in_), func, bias=bias, scale=scale)
+        return add("a", emit, regs(in_), wr, c)
+
+    def mm(groups, part=(True, True)):
+        first, final = part
+        rd, wr, c, m = [], [], 0.0, 0
+        for out, lst in groups:
+            wr += regs(out)
+            for l, r in lst:
+                rd += regs(l, r)
+                m += 1
+                c += max(64, cnt(r)) * (4 if SCRATCH[r[0]][2] == "float32" else 1)
+
+        def emit():
+            last = None
+            for out, lst in groups:
+                for k, (l, r) in enumerate(lst):
+                    last = g.tensor.matmul(ap(out), ap(l), ap(r), first and k == 0, final and k == len(lst) - 1)
+            return last
+        return add("t", emit, sorted(set(rd)), wr, ("t", c, m))
+
+    def gp(fn, rd, wr, c):
+        return add("g", fn, regs(*rd), regs(*wr), c)
+
+    def M128(name):
+        return V(name, 0, 128)
+
+    for k in range(4):
+        a, b = 1024 * k, 1024 * (k + 1)
+        add("s" if k % 2 else "s2", (lambda a=a, b=b, k=k: (g.sync if k % 2 else g.scalar).dma_start(T.X[:, a:b], T.xt[:, a:b])), [], [R("X", a, b)], 1500.0, "x%d" % k, 16)
+    for j in range(NCH):
+        o, n = OFF[j], CH[j]
+        add("s", (lambda o=o, n=n: g.sync.dma_start(T.li[:, 2 * o:2 * o + n], T.ba[:, o:o + n])), [], [R("li", 2 * o, 2 * o + n)], 1500.0, "la%d" % j, 16)
+        add("s", (lambda o=o, n=n: g.sync.dma_start(T.li[:, 2 * o + n:2 * o + 2 * n], T.bb[:, o:o + n])), [], [R("li", 2 * o + n, 2 * o + 2 * n)], 1500.0, "la%d" % j, 16)
+        add("s", (lambda o=o, n=n: g.sync.dma_start(T.mz0[:, 3 * o:3 * o + n], T.zp[:, o:o + n])), [], [R("mz0", 3 * o, 3 * o + n)], 1500.0, "la%d" % j, 16)
+    add("s", lambda: g.sync.dma_start(T.wcol[:], T.wl[:]), [], [R("wcol", 0, 1)], 1500.0, "lw", 16)
+    for k in ops:
+        if k["sem"] is not None and k["sem"].startswith("la"):
+            k["need"] = 48
+
+    fill(V("ones", 0, 144), 1.0)
+    gp(lambda: g.iota(T.bi[:, 0:16], [[0, 16]], 0, 16), [], [V("bi", 0, 16)], 200.0)
+    gp(lambda: g.iota(T.bi[:, 16:32], [[256, 16]], 0, 0), [], [V("bi", 16, 32)], 200.0)
+    W9 = V("ones", 0, 144)
+    gp(lambda: g.affine_select(T.tmpw[:], T.ones[:], [[-16, 9], [0, 16]], ALU.is_ge, 0.0, 0, 1), [W9], [V("tmpw", 0, 144)], 450.0)
+    gp(lambda: g.affine_select(T.tmpw2[:], T.tmpw[:], [[16, 9], [0, 16]], ALU.is_ge, 0.0, 15, -1), [V("tmpw", 0, 144)], [V("tmpw2", 0, 144)], 450.0)
+    cp(M128("GBb"), V("tmpw2", 0, 128))
+    gp(lambda: g.affine_select(T.Ib[:], T.GBb[:], [[1, 128]], ALU.is_equal, 0.0, 0, -1), [M128("GBb")], [M128("Ib")], 450.0)
+    gp(lambda: g.affine_select(T.Eb[:], T.tmpw2[:], [[0, 9], [1, 16]], ALU.is_equal, 0.0, -15, 0), [V("tmpw2", 0, 144)], [V("Eb", 0, 144)], 450.0)
+    gp(lambda: g.affine_select(T.Tr1[:], T.GBb[:], [[1, 128]], ALU.is_ge, 0.0, -1, -1), [M128("GBb")], [M128("Tr1")], 450.0)
+    for nm, c in (("H1", 1.0), ("Hn", -1.0), ("H65", 65.0), ("H101", 101.0), ("H2048", 2048.0), ("Ibn", -1.0), ("Ib128", 128.0), ("Ibh", 0.5), ("H256", 256.0), ("F1", 1.0)):
+        ts(M128(nm), M128("Ib"), c, ALU.mult)
+    ts(M128("TrS"), M128("Tr1"), 0.21875, ALU.mult)
+    cp(V("on16", 0, NM), V("ones", 0, NM))
+    fill(V("RST", 0, 16 * NM), 1.0)
+    add("v", lambda: g.vector.memset(T.RST[:, 0:16 * NM:16], 0.0), [], [R("RST", 0, 16 * NM)], cv(NM))
+    for p in range(2):
+        act(V("zs%d" % p, 0, 16 * NM), V("RST", 0, 16 * NM), ACT.Copy, scale=0.0)
+    ts(V("Ew", 0, 144), V("Eb", 0, 144), V("wcol", 0, 1), ALU.mult)
+    fill(M128("FK"), -1.0 / 32)
+    ts(M128("Wb"), M128("GBb"), V("wcol", 0, 1), ALU.mult)
+    ts(V("bi", 0, 16), V("bi", 0, 16), 255, ALU.bitwise_and)
+    tt(V("base", 0, 16), V("bi", 0, 16), V("bi", 16, 32), ALU.add)
+
+    def E(b, nm="Eb"):
+        return V(nm, 15 - b, 15 - b + 128)
+
+    nxt, prv = T.cores[(rank + 1) % len(T.cores)], T.cores[(rank - 1) % len(T.cores)]
+    sends = {}
+    X = V("X", 0, 4096)
+
+    def names(t, j):
+        q = t * NCH + j
+        p, o, n = q % NB, OFF[j], CH[j]
+        e = 16 * n
+        D = {"q": q, "p": p, "o": o, "n": n, "e": e}
+        for nm in ("zr", "h", "do", "dc", "ah", "ao", "ac", "ch", "rm"):
+            D[nm] = V("%s%d" % (nm, p), 0, e)
+
+        def slot(base, k, w=None):
+            return V("%s%d" % (base, p), k * NM, k * NM + (w or n))
+        for k, nm in enumerate(("dhs", "m1", "t1", "De", "chf", "jd", "sOm", "ym")):
+            D[nm] = slot("f", k)
+        for k, nm in enumerate(("rec", "w0", "wa", "am", "sg", "J", "sp", "nIo", "Gno")):
+            D[nm] = slot("b", k)
+        D["HO"] = V("s%d" % p, 0, 2 * n)
+        D["Hc"], D["Oc"] = V("s%d" % p, 0, n), V("s%d" % p, n, 2 * n)
+        D["stl"], D["Cc"] = slot("s", 2), slot("s", 3)
+        D["pm"], D["r"], D["p2"] = slot("i", 0), slot("i", 1), slot("i", 2)
+        D["Cu"], D["chu"] = slot("u", 0), slot("u", 1)
+        lu, mz = "lu%d" % t, "mz%d" % t
+        D["LU"] = V(lu, 2 * o, 2 * o + 2 * n)
+        D["Hu"], D["Ou"] = V(lu, 2 * o, 2 * o + n), V(lu, 2 * o + n, 2 * o + 2 * n)
+        D["z"], D["nI"], D["G"] = [V(mz, 3 * o + k * n, 3 * o + (k + 1) * n) for k in range(3)]
+        if t < READS - 1:
+            su, sz = "su%d" % t, "sz%d" % t
+            D["Hs"], D["Os"] = V(su, 2 * o + n, 2 * o + 2 * n), V(su, 2 * o, 2 * o + n)
+            D["zn"], D["nIn"], D["Gn"] = [V(sz, 3 * o + k * n, 3 * o + (k + 1) * n) for k in range(3)]
+            if t == 0:
+                D["J"] = D["nIn"]
+        else:
+            D["nIn"] = D["nIo"]
+            D["Gn"] = D["Gno"]
+
+        def ps(bk, k):
+            return V("p%d" % bk, k * n, k * n + n)
+        lb, db = 4 + q % 2, 2 + q % 2
+        for nm, k in (("OmH", 0), ("CmH", 1), ("Op", 2), ("HS", 2), ("S", 3), ("Y", 3), ("bp", 3), ("Hr", 4), ("sOp", 4)):
+            D[nm] = ps(lb, k)
+        for nm, k in (("dh", 0), ("ddo", 1), ("ddc", 2), ("RG", 3), ("pf", 4), ("t2", 0), ("up", 2), ("zM", 3), ("sc", 4)):
+            D[nm] = ps(db, k)
+        D["UL"] = V("p%d" % db, 480, 480 + n // 16)
+        for nm, k in (("Vp", 0), ("X1", 1), ("X2", 2), ("H2", 3), ("S2", 4)):
+            D[nm] = ps(6 + q % 2, k)
+        return D
+
+    I1, In, F1 = M128("Ib"), M128("Ibn"), M128("F1")
+    H1, Hn = M128("H1"), M128("Hn")
+
+    def cut(n, w):
+        m = max(1, (n + w - 1) // w)
+        s = [2 * (n // 2 * i // m) for i in range(m + 1)]
+        return list(zip(s[:-1], s[1:]))
+
+    def sub(v, a, b, k=1):
+        return V(v[0], v[1] + k * a, v[1] + k * b)
+
+    def pre(t, j):
+        phase("pre", j)
+        D = names(t, j)
+        n = D["n"]
+        if t == 0:
+            li = V("li", 2 * D["o"], 2 * D["o"] + 2 * n)
+            cp(D["LU"], li)
+            ts(D["HO"], li, -2048.0, ALU.add)
+        else:
+            for nm, v in (("rl", D["LU"]), ("rz", V(D["z"][0], 3 * D["o"], 3 * D["o"] + 3 * n))):
+                k = add("n", None, [], regs(v), ("net", 0), "%s%d_%d" % (nm, t, j), NENG, after=[sends[(nm, t - 1, j)]])
+                ops[k]["soft"] = True
+            ts(D["HO"], D["LU"], -2048.0, ALU.add)
+        on = V("on16", 0, n)
+        mm([(D["Op"], [(H1, D["Oc"])]), (D["S"], [(M128("H65"), D["Hc"]), (M128("H101"), D["Oc"])]),
+            (D["OmH"], [(H1, D["Oc"]), (Hn, D["Hc"])]), (D["Hr"], [(H1, D["Hc"]), (M128("H2048"), on)])])
+        tt(D["pm"], D["Hc"], D["Op"], ALU.mult)
+        ts(D["pm"], D["pm"], 5, ALU.arith_shift_right)
+        tt(D["pm"], D["pm"], D["S"], ALU.add)
+        ts(D["pm"], D["pm"], 4095, ALU.bitwise_and)
+        cp(D["Cu"], D["pm"])
+        ts(D["stl"], D["OmH"], 0.0, ALU.is_equal)
+        tt(D["HS"], D["stl"], D["Hr"], ALU.mult)
+        ts(D["Cc"], D["pm"], -2048.0, ALU.add)
+        mm([(D["CmH"], [(H1, D["Cc"]), (Hn, D["Hc"])])])
+        zs = "zs%d" % (D["q"] % 2)
+        add("v", lambda: g.vector.tensor_copy(T[zs][:, 0:D["e"]:16], ap(D["z"])), regs(D["z"]), [R(zs, 0, D["e"])], cv(n, 0.5))
+        for a in range(0, D["e"], 512):
+            scan(V(D["zr"][0], a, a + 512), V("RST", a, a + 512), V(zs, a, a + 512), ALU.mult, ALU.add)
+
+    def s1(t, j):
+        D = names(t, j)
+        n, e = D["n"], D["e"]
+        phase("s1", j)
+        for a, b in cut(n, PH):
+            act(sub(D["h"], a, b, 16), ind(X, sub(D["Hu"], a, b)), ACT.Copy)
+        for dst, lst in (("do", "Ou"), ("dc", "Cu")):
+            for a, b in cut(n, PD):
+                tt(sub(D[dst], a, b, 16), ind(X, sub(D[lst], a, b)), sub(D["zr"], a, b, 16), ALU.subtract)
+        for k in range(n // 32):
+            a, b = 512 * k, 512 * k + 512
+            bk = V("p%d" % (k % 2), 0, 512)
+            mm([(bk, [(I1, V(D["h"][0], a, b)), (In, V(D["zr"][0], a, b))])])
+            act(V(D["ah"][0], a, b), bk, ACT.Abs)
+        for src, dst in (("do", "ao"), ("dc", "ac")):
+            for a, b in cut(n, PD):
+                act(sub(D[dst], a, b, 16), sub(D[src], a, b, 16), ACT.Abs)
+        for src, dst in (("ah", "dh"), ("ao", "ddo"), ("ac", "ddc")):
+            mm([(D[dst], [(E(b), V(D[src][0], b, e, 16)) for b in range(16)])])
+
+    def choice(t, j):
+        D = names(t, j)
+        n, e = D["n"], D["e"]
+        phase("ch", j)
+        cp(D["dhs"], D["dh"]) if DHV else act(D["dhs"], D["dh"], ACT.Copy)
+        tt(D["m1"], D["dhs"], D["ddc"], ALU.min)
+        tt(D["rec"], D["m1"], D["ddo"], ALU.is_ge)
+        tt(D["w0"], D["dhs"], D["ddc"], ALU.is_gt)
+        hb = M128("Ibh")
+        mm([(D["RG"], [(H1, D["stl"])] + ([(hb, D["G"]), (hb, V("ones", 0, n))] if t else []) + [(I1, D["rec"])])])
+        tt(D["t1"], D["rec"], D["OmH"], ALU.mult)
+        tt(D["wa"], D["w0"], D["RG"], ALU.is_gt)
+        mm([(D["pf"], [(M128("TrS"), D["wa"])])])
+        tt(D["am"], D["wa"], D["pf"], ALU.is_gt)
+        tt(D["t2"], D["am"], D["CmH"], ALU.mult)
+        tt(D["De"], D["t1"], D["t2"], ALU.add)
+        tt(D["chf"], D["De"], D["Hr"], ALU.add)
+        cp(D["chu"], D["chf"])
+        mm([(D["Vp"], [(In, V(D["h"][0], b, e, 16)) for b in range(16)])], (True, False))
+        for a, b in cut(n, PC):
+            act(sub(D["ch"], a, b, 16), ind(X, sub(D["chu"], a, b)), ACT.Copy)
+
+    def upd(t, j):
+        D = names(t, j)
+        n, e, o = D["n"], D["e"], D["o"]
+        phase("up", j)
+        for a, b in cut(n, PC):
+            scan(sub(D["rm"], a, b, 16), V("RST", 16 * a, 16 * b), sub(D["ch"], a, b, 16), ALU.mult, ALU.max)
+        k = n // 16
+        c0 = o // 16
+        U0, U1 = V("ul", c0, c0 + k), V("ul", 16 + c0, 16 + c0 + k)
+        nl = V("nl", c0, c0 + k)
+        if t < READS - 1:
+            mm([(D["UL"], [(E(r, "Ew"), V(D["rm"][0], 16 * r + 15, e, 256)) for r in range(16)])])
+            cp(U0, D["UL"])
+            ts(U1, U0, 15, ALU.bitwise_and)
+            tt(U1, U1, V("base", c0, c0 + k), ALU.add)
+            cp(nl, U1)
+            xv = V("xv", o, o + n)
+            tt(xv, ind(X, nl), V(D["rm"][0], 15, e, 16), ALU.add)
+            ts(xv, xv, 1, ALU.arith_shift_right)
+            mm([(D["zM"], [(I1, D["z"]), (In, V(D["rm"][0], 15, e, 16))])])
+            act(D["zn"], D["zM"], ACT.Abs)
+        mm([(D["up"], [(M128("Wb"), V(D["rm"][0], 15, e, 16))])])
+        cp(D["p2"], D["up"])
+        ts(D["p2"], D["p2"], 4095, ALU.bitwise_and)
+        tt(D["p2"], D["p2"], D["HS"], ALU.mult)
+        ts(D["p2"], D["p2"], 5, ALU.arith_shift_right)
+
+    def scat(t, o, n):
+        phase("sc", o)
+        cp(ind(X, V("nl", o // 16, (o + n) // 16)), V("xv", o, o + n))
+
+    def vote(t, j):
+        D = names(t, j)
+        n, e, o = D["n"], D["e"], D["o"]
+        phase("vo", j)
+        mm([(D["Vp"], [(I1, V(D["ch"][0], b, e, 16)) for b in range(16)])], (False, True))
+        act(D["sg"], D["Vp"], ACT.Sign, bias=0.5)
+        GB = M128("GBb")
+        gr = [(D["X1"], [(GB, D["sg"]), (M128("Ib128"), D["rec"]), (M128("Ib128"), D["am"]), (M128("H256"), D["stl"])]),
+              (D["X2"], [(GB, D["sg"]), (M128("Ib128"), D["am"])] + ([(M128("Ib128"), D["G"])] if t else []))]
+        if t < READS - 1:
+            gr.append((D["sc"], [(GB, D["sg"])]))
+        mm(gr)
+        ts(D["J"], D["X1"], 126.0, ALU.is_ge)
+        act(D["Gn"], D["X2"], ACT.Sign, bias=3.0 if t else -125.0)
+        if t < READS - 1:
+            act(V("junk", 0, n), D["sc"], ACT.Sign, bias=3.0, acc=V("kacc", 8 * (t % 2) + j, 8 * (t % 2) + j + 1))
+        tt(D["jd"], D["J"], D["De"], ALU.mult)
+        if t:
+            mm([(D["Y"], [(I1, D["nI"]), (I1, D["J"])])])
+            act(D["sp"], D["Y"], ACT.Relu, bias=1.0, scale=-1.0)
+            act(D["nIn"], D["Y"], ACT.Square, bias=1.0, scale=-1.0)
+            mm([(D["bp"], [(M128("Tr1"), D["sp"])])])
+            tt(D["r"], D["sp"], D["bp"], ALU.mult)
+            ts(D["r"], D["r"], 1, ALU.bitwise_and)
+            tt(D["sOp"], D["r"], D["CmH"], ALU.mult)
+            tt(D["sOm"], D["sp"], D["OmH"], ALU.mult)
+            tt(D["jd"], D["jd"], D["sOp"], ALU.add)
+            tt(D["ym"], D["sOp"], D["sOm"], ALU.subtract)
+
+    def post(t, j):
+        D = names(t, j)
+        n, e, o = D["n"], D["e"], D["o"]
+        k, c0 = n // 16, o // 16
+        phase("po", j)
+        on = V("on16", 0, n)
+        L = [(H1, D["Hc"]), (F1, D["jd"])]
+        L2 = [(H1, D["Oc"]), (M128("H2048"), on)]
+        if t:
+            L2 += [(M128("HK"), D["stl"]), (F1, D["ym"])]
+        mm([(D["H2"], L), (D["S2"], L2)])
+        if t < READS - 1:
+            ts(D["Hs"], D["H2"], 2048.0, ALU.add)
+        else:
+            ts(V("oyb", o, o + n), D["H2"], 2048.0, ALU.add)
+        tt(D["p2"], D["p2"], D["S2"], ALU.add)
+        ts(D["p2"], D["p2"], 4095, ALU.bitwise_and)
+        if t < READS - 1:
+            cp(D["Os"], D["p2"])
+            su, sz = "su%d" % t, "sz%d" % t
+            rid, pid = topo.addr(nxt, core)
+            mask = sum(1 << x for x in topo.engines(core, nxt)[:NENG])
+            lu, mz = "lu%d" % (t + 1), "mz%d" % (t + 1)
+
+            def snd(src, dst, a, b, sem):
+                return lambda: g.remote_dma(T[dst][:, a:b], T[src][:, a:b], T.sem[sem], T.sem.left, pid, rid, mask)
+            sends[("rz", t, j)] = add("g", snd(sz, mz, 3 * o, 3 * o + 3 * n, "rz%d_%d" % (t + 1, j)), [R(sz, 3 * o, 3 * o + 3 * n)], [], 300.0, "left", NENG)
+            sends[("rl", t, j)] = add("g", snd(su, lu, 2 * o, 2 * o + 2 * n, "rl%d_%d" % (t + 1, j)), [R(su, 2 * o, 2 * o + 2 * n)], [], 300.0, "left", NENG)
+        else:
+            cp(V("oya", o, o + n), D["p2"])
+            act(V("oyi", o, o + n), D["nIn"], ACT.Identity, bias=1.0, scale=-1.0)
+            act(V("oyg", o, o + n), D["Gn"], ACT.Identity, bias=0.5, scale=0.5)
+            for m, (src, dst) in enumerate((("oya", "ya"), ("oyb", "yb"), ("oyi", "yi"), ("oyg", "yg"))):
+                add("s", (lambda src=src, dst=dst: g.sync.dma_start(T[dst][:, o:o + n], T[src][:, o:o + n])), [R(src, o, o + n)], [], 200.0, "out%d" % (4 * j + m), 16)
+
+    def kcalc(t):
+        phase("kc", 0)
+        b = 8 * (t % 2)
+        kb = "p%d" % (2 + (t * NCH + NCH - 1) % 2)
+        mm([(V(kb, 500, 501), [(M128("FK"), V("kacc", b + j, b + j + 1)) for j in range(NCH)])])
+        ts(V("kcol", 0, 1), V(kb, 500, 501), 1024.0, ALU.add)
+        ts(M128("HK"), M128("H1"), V("kcol", 0, 1), ALU.mult)
+
+    pre(0, 0)
+    for t in range(READS):
+        for j in range(NCH):
+            if t == 0 and j + 1 < NCH:
+                pre(0, j + 1)
+            s1(t, j)
+            if t and j + 1 < NCH:
+                pre(t, j + 1)
+            choice(t, j)
+            if j == NCH - 1 and t < READS - 1 and NCH > 1:
+                scat(t, 0, OFF[j])
+            upd(t, j)
+            if j == NCH - 1:
+                if t < READS - 1:
+                    scat(t, OFF[j], CH[j])
+                    pre(t + 1, 0)
+            vote(t, j)
+            post(t, j)
+        if t < READS - 1:
+            kcalc(t)
+
+    order, fin = schedule(ops, EST, BONUS)
+    N = len(ops)
+
+    eng = {"v": g.vector, "t": g.tensor, "a": g.scalar, "g": g, "s": g.sync, "s2": g.scalar}
+    own = {"v": "qv", "t": "qt", "a": "qa", "g": "qg"}
+    phys = {"s2": "a"}
+    total = {}
+    clk = {q: {} for q in ("v", "t", "a", "g", "s")}
+    val = [None] * N
+    opclk = [None] * N
+    for k in order:
+        o = ops[k]
+        q = phys.get(o["q"], o["q"])
+        if q == "n":
+            val[k] = (o["sem"], o["inc"])
+            opclk[k] = {o["sem"]: o["inc"]}
+            total[o["sem"]] = o["inc"]
+            continue
+        c = clk[q]
+        ds = [d for d, w in o["deps"].items() if w and ops[d]["sem"] != "left"]
+        ds.sort(key=lambda d: -fin[d])
+        for d in ds:
+            s, v = val[d]
+            if c.get(s, 0) < v:
+                eng[q].wait_ge(T.sem[s], v)
+                for s2, v2 in opclk[d].items():
+                    if c.get(s2, 0) < v2:
+                        c[s2] = v2
+        ins = o["fn"]()
+        s = o["sem"] or own[q]
+        total[s] = total.get(s, 0) + o["inc"]
+        if s != "left":
+            ins.then_inc(T.sem[s], o["inc"])
+        val[k] = (s, o.get("need", total[s]))
+        opclk[k] = dict(c)
+        if s != "left":
+            opclk[k][s] = val[k][1]
+    for s in sorted(total):
+        g.wait_ge(T.sem[s], total[s])

@@ -7,7 +7,8 @@ NM = max(CH)
 NB = 3
 READS = 4
 NENG = 8
-PH, PD, PC, DHV = 48, 96, 96, False
+RELU = [(), (), ()]
+PH, PD, PC, DHV = 48, 48, 48, True
 
 SCRATCH = {
     "X": ("sbuf", [128, 4096], "bfloat16"),
@@ -21,10 +22,13 @@ SCRATCH = {
     "tmpw": ("sbuf", [128, 144], "bfloat16"), "tmpw2": ("sbuf", [128, 144], "bfloat16"),
     "tmpt": ("sbuf", [128, 128], "bfloat16"),
     "H1": ("sbuf", [128, 128], "float16"), "Hn": ("sbuf", [128, 128], "float16"),
-    "H65": ("sbuf", [128, 128], "float16"), "H101": ("sbuf", [128, 128], "float16"),
+    "H2080": ("sbuf", [128, 128], "float16"), "H3232": ("sbuf", [128, 128], "float16"),
+    "H32": ("sbuf", [128, 128], "float16"), "m96": ("sbuf", [128, NM], "float16"),
+    "F32": ("sbuf", [128, 128], "float32"), "F32n": ("sbuf", [128, 128], "float32"),
     "H2048": ("sbuf", [128, 128], "float16"), "H256": ("sbuf", [128, 128], "float16"),
     "HK": ("sbuf", [128, 128], "float16"), "on16": ("sbuf", [128, NM], "float16"),
     "F1": ("sbuf", [128, 128], "float32"), "FK": ("sbuf", [128, 128], "float32"),
+    "E2": ("sbuf", [128, 144], "bfloat16"), "En": ("sbuf", [128, 144], "bfloat16"),
     "Wb": ("sbuf", [128, 128], "bfloat16"),
     "bi": ("sbuf", [128, 32], "int32"), "base": ("sbuf", [128, 16], "int32"),
     "RST": ("sbuf", [128, 16 * NM], "bfloat16"),
@@ -60,8 +64,13 @@ SEMAPHORES += ["rl%d_%d" % (t, j) for t in range(1, READS) for j in range(NCH)]
 SEMAPHORES += ["rz%d_%d" % (t, j) for t in range(1, READS) for j in range(NCH)]
 SEMAPHORES += ["out%d" % k for k in range(4 * NCH)]
 
-EST = {"cy": 1.0, "gam": 1.56, "scat": 3.0, "pec": 0.5, "fv": 10.0, "fa": 10.0, "ft": 5.0, "wake": 60.0, "net": 3500.0, "dma": 2000.0, "iss": 500.0}
+EST = {"cy": 1.0, "gam": 1.56, "scat": 3.0, "pec": 0.5, "fv": 0.0, "fa": 0.0, "ft": 0.0, "wake": 80.0, "net": 6500.0, "dma": 2000.0, "iss": 500.0}
+SHIFT = {'s12': '5:-56 16:123 13:-23 3:-20 8:-37 9:102 14:-23 2:-20 x:-8 6:25 4:4 15:20', 's11': '9:-22 12:208 10:-58 18:36 14:-14 6:-7 13:-23 1:-35 7:12 17:45 0:-12 5:-8 11:12 16:-1 x:-1 15:19 8:-24', 'ch2': '2:-22 13:111 x:-159 12:57 5:-37 0:-40 4:-12 1:-8 11:76 8:17 14:15 3:-53 9:-5', 'vo0': '10:-47 11:139 13:-44 2:69 8:39 12:43 0:-144 15:-6 3:5 9:9 6:20 5:6 7:1 x:1 1:33', 'vo2': '1:40 10:129 14:-103 0:93 8:-32 11:-46 12:16 3:98 15:-43 2:6 5:4 13:-5 7:15 6:-5 9:-7 4:-27', 'ch1': 'x:1 12:5 1:115 0:38 13:-66 6:-51 14:16 5:-35 9:-31 8:-12 4:15 7:17 3:36 11:7', 'ch0': '13:22 14:1 1:84 0:1 6:16 12:213 8:72 x:9 4:39 3:-7 7:16 9:-2', 'c': '19:24 5:22 27:51 26:-14 40:23 37:128 43:22 1:-71 39:94 9:-65 25:-18 4:55 38:-36 30:22 33:-73 42:-17 29:-154 10:60 12:80 23:-11 2:132 0:-95 17:-13 11:11 41:1 7:-21 49:20 6:32 15:19 14:4 48:35 28:1 45:-15 20:36 3:-24 44:-8 8:29 18:-13 22:-26', 'kc0': '2:-2 1:-8 x:-286 0:-23', 'pre0': '13:-16 12:48 5:-12 3:128 8:-3 10:-34 1:-44 x:-1 0:-29', 'pre2': '7:-64 12:-19 2:-21 8:-43 6:-2 1:27 0:-22 x:-4 10:-14 3:-12 13:-8', 'up2': '7:29 6:-8 x:24 8:-33 1:-21 9:-150 0:-12 10:-75 12:-11 3:15 4:26 14:10 5:-7', 'up1': '10:4 14:-122 x:101 1:164 4:-110 6:-25 12:46 11:2 9:-36 3:-6 8:-11 0:5 2:33', 'up0': '14:-82 9:10 2:28 5:-45 8:-91 0:-6 6:-132 13:25 3:-29 11:107 12:-7', 'po0': '6:-12 0:54 8:-23 5:-10 7:57 4:40 9:-38 10:54 3:35 x:14', 'pre1': '1:-16 7:4 4:4 5:71 12:42 9:1 3:1 11:-1 0:-15', 'vo1': '15:-72 x:54 11:-15 13:20 12:-52 14:-37 8:-43 9:132 4:-102 0:-55 10:-24 7:12 6:-35 1:-32 2:-52 5:51 3:19', 'po1': '0:33 9:63 7:23 1:12 5:-78 3:-3 x:3 4:-24 8:-6 10:-46 2:16', 's10': '5:118 0:110 13:40 3:-30 2:-12 12:-15 16:62 11:-7 15:-7 9:3 17:-35 6:-99 7:4 14:59', 'po2': '5:11 2:-4 7:25 10:-50 6:-55 x:29 4:41 9:11 1:-16 3:22 8:74 0:2', 'sc192': '0:88 x:4', 'sc0': '0:-11 x:-10'}
 BONUS = {}
+for _p, _s in SHIFT.items():
+    for _e in _s.split():
+        _i, _v = _e.split(":")
+        BONUS[_p if _i == "x" else _p + ":" + _i] = 100.0 * int(_v)
 
 
 def price(w, E):
@@ -100,7 +109,7 @@ def schedule(ops, E, bonus):
     bot = [0.0] * N
     for k in range(N - 1, -1, -1):
         bot[k] = cost[k] + W + max([bot[s] for s in succ[k]] + [0.0])
-    pri = [bot[k] + bonus.get(ops[k]["tag"], 0.0) for k in range(N)]
+    pri = [bot[k] + bonus.get(ops[k]["tag"], 0.0) + bonus.get(ops[k]["tag"].split(":")[0], 0.0) for k in range(N)]
     left = [len(o["deps"]) for o in ops]
     ready, free, order = {}, {}, []
     rt, fin = [0.0] * N, [0.0] * N
@@ -126,7 +135,7 @@ def schedule(ops, E, bonus):
         order.append(k)
         for s in succ[k]:
             left[s] -= 1
-            rt[s] = max(rt[s], fin[k] + W)
+            rt[s] = max(rt[s], fin[k] + (W if ops[s]["deps"][k] else 0.0))
             if left[s] == 0:
                 ready[ops[s]["q"]].append(s)
     return order, fin
@@ -299,16 +308,19 @@ def rank_program(g, core, T, topo):
     gp(lambda: g.affine_select(T.Ib[:], T.GBb[:], [[1, 128]], ALU.is_equal, 0.0, 0, -1), [M128("GBb")], [M128("Ib")], 450.0)
     gp(lambda: g.affine_select(T.Eb[:], T.tmpw2[:], [[0, 9], [1, 16]], ALU.is_equal, 0.0, -15, 0), [V("tmpw2", 0, 144)], [V("Eb", 0, 144)], 450.0)
     gp(lambda: g.affine_select(T.Tr1[:], T.GBb[:], [[1, 128]], ALU.is_ge, 0.0, -1, -1), [M128("GBb")], [M128("Tr1")], 450.0)
-    for nm, c in (("H1", 1.0), ("Hn", -1.0), ("H65", 65.0), ("H101", 101.0), ("H2048", 2048.0), ("Ibn", -1.0), ("Ib128", 128.0), ("Ibh", 0.5), ("H256", 256.0), ("F1", 1.0)):
+    for nm, c in (("H1", 1.0), ("Hn", -1.0), ("H2080", 2080.0), ("H3232", 3232.0), ("H32", 32.0), ("F32", 32.0), ("F32n", -32.0), ("H2048", 2048.0), ("Ibn", -1.0), ("Ib128", 128.0), ("Ibh", 0.5), ("H256", 256.0), ("F1", 1.0)):
         ts(M128(nm), M128("Ib"), c, ALU.mult)
     ts(M128("TrS"), M128("Tr1"), 0.21875, ALU.mult)
     cp(V("on16", 0, NM), V("ones", 0, NM))
+    ts(V("m96", 0, NM), V("ones", 0, NM), -96.0, ALU.mult)
     fill(V("RST", 0, 16 * NM), 1.0)
     add("v", lambda: g.vector.memset(T.RST[:, 0:16 * NM:16], 0.0), [], [R("RST", 0, 16 * NM)], cv(NM))
     for p in range(2):
         act(V("zs%d" % p, 0, 16 * NM), V("RST", 0, 16 * NM), ACT.Copy, scale=0.0)
     ts(V("Ew", 0, 144), V("Eb", 0, 144), V("wcol", 0, 1), ALU.mult)
-    fill(M128("FK"), -1.0 / 32)
+    ts(V("E2", 0, 144), V("Eb", 0, 144), 2.0, ALU.mult)
+    ts(V("En", 0, 144), V("Eb", 0, 144), -1.0, ALU.mult)
+    fill(M128("FK"), -0.5)
     ts(M128("Wb"), M128("GBb"), V("wcol", 0, 1), ALU.mult)
     ts(V("bi", 0, 16), V("bi", 0, 16), 255, ALU.bitwise_and)
     tt(V("base", 0, 16), V("bi", 0, 16), V("bi", 16, 32), ALU.add)
@@ -330,7 +342,7 @@ def rank_program(g, core, T, topo):
 
         def slot(base, k, w=None):
             return V("%s%d" % (base, p), k * NM, k * NM + (w or n))
-        for k, nm in enumerate(("dhs", "m1", "t1", "De", "chf", "jd", "sOm", "ym")):
+        for k, nm in enumerate(("dhs", "m1", "t1", "De", "jd", "sOm", "sO", "chf")):
             D[nm] = slot("f", k)
         for k, nm in enumerate(("rec", "w0", "wa", "am", "sg", "J", "sp", "nIo", "Gno")):
             D[nm] = slot("b", k)
@@ -355,14 +367,14 @@ def rank_program(g, core, T, topo):
 
         def ps(bk, k):
             return V("p%d" % bk, k * n, k * n + n)
-        lb, db = 4 + q % 2, 2 + q % 2
-        for nm, k in (("OmH", 0), ("CmH", 1), ("Op", 2), ("HS", 2), ("S", 3), ("Y", 3), ("bp", 3), ("Hr", 4), ("sOp", 4)):
+        lb, db = 4 + q % 3, 2 + q % 2
+        for nm, k in (("OmH", 0), ("CmH", 1), ("Op", 2), ("HS", 2), ("S", 3), ("Y", 3), ("bp", 3), ("Hr", 4)):
             D[nm] = ps(lb, k)
-        for nm, k in (("dh", 0), ("ddo", 1), ("ddc", 2), ("RG", 3), ("pf", 4), ("t2", 0), ("up", 2), ("zM", 3), ("sc", 4)):
+        for nm, k in (("dh", 0), ("ddo", 1), ("ddc", 2), ("RG", 3), ("pf", 4), ("cp", 1), ("up", 2), ("zM", 3)):
             D[nm] = ps(db, k)
         D["UL"] = V("p%d" % db, 480, 480 + n // 16)
-        for nm, k in (("Vp", 0), ("X1", 1), ("X2", 2), ("H2", 3), ("S2", 4)):
-            D[nm] = ps(6 + q % 2, k)
+        for nm, k in (("Vp", 0), ("X1", 1), ("X2", 2), ("sc", 3), ("H2", 3), ("S2", 4)):
+            D[nm] = ps(7, k)
         return D
 
     I1, In, F1 = M128("Ib"), M128("Ibn"), M128("F1")
@@ -390,17 +402,15 @@ def rank_program(g, core, T, topo):
                 ops[k]["soft"] = True
             ts(D["HO"], D["LU"], -2048.0, ALU.add)
         on = V("on16", 0, n)
-        mm([(D["Op"], [(H1, D["Oc"])]), (D["S"], [(M128("H65"), D["Hc"]), (M128("H101"), D["Oc"])]),
+        mm([(D["Op"], [(H1, D["Oc"])]), (D["S"], [(M128("H2080"), D["Hc"]), (M128("H3232"), D["Oc"])]),
             (D["OmH"], [(H1, D["Oc"]), (Hn, D["Hc"])]), (D["Hr"], [(H1, D["Hc"]), (M128("H2048"), on)])])
         tt(D["pm"], D["Hc"], D["Op"], ALU.mult)
-        ts(D["pm"], D["pm"], 5, ALU.arith_shift_right)
         tt(D["pm"], D["pm"], D["S"], ALU.add)
-        ts(D["pm"], D["pm"], 4095, ALU.bitwise_and)
+        ts(D["pm"], D["pm"], 5, ALU.arith_shift_right, 4095, ALU.bitwise_and)
         cp(D["Cu"], D["pm"])
         ts(D["stl"], D["OmH"], 0.0, ALU.is_equal)
         tt(D["HS"], D["stl"], D["Hr"], ALU.mult)
-        ts(D["Cc"], D["pm"], -2048.0, ALU.add)
-        mm([(D["CmH"], [(H1, D["Cc"]), (Hn, D["Hc"])])])
+        tt(D["CmH"], D["pm"], D["Hr"], ALU.subtract)
         zs = "zs%d" % (D["q"] % 2)
         add("v", lambda: g.vector.tensor_copy(T[zs][:, 0:D["e"]:16], ap(D["z"])), regs(D["z"]), [R(zs, 0, D["e"])], cv(n, 0.5))
         for a in range(0, D["e"], 512):
@@ -422,9 +432,16 @@ def rank_program(g, core, T, topo):
             act(V(D["ah"][0], a, b), bk, ACT.Abs)
         for src, dst in (("do", "ao"), ("dc", "ac")):
             for a, b in cut(n, PD):
-                act(sub(D[dst], a, b, 16), sub(D[src], a, b, 16), ACT.Abs)
-        for src, dst in (("ah", "dh"), ("ao", "ddo"), ("ac", "ddc")):
-            mm([(D[dst], [(E(b), V(D[src][0], b, e, 16)) for b in range(16)])])
+                if src in RELU[j]:
+                    ts(sub(D[dst], a, b, 16), sub(D[src], a, b, 16), 0.0, ALU.max)
+                else:
+                    act(sub(D[dst], a, b, 16), sub(D[src], a, b, 16), ACT.Abs)
+        for raw, src, dst in ((None, "ah", "dh"), ("do", "ao", "ddo"), ("dc", "ac", "ddc")):
+            if raw in RELU[j]:
+                mm([(D[dst], [(E(b, "En"), V(D[raw][0], b, e, 16)) for b in range(16)] +
+                     [(E(b, "E2"), V(D[src][0], b, e, 16)) for b in range(16)])])
+            else:
+                mm([(D[dst], [(E(b), V(D[src][0], b, e, 16)) for b in range(16)])])
 
     def choice(t, j):
         D = names(t, j)
@@ -440,11 +457,10 @@ def rank_program(g, core, T, topo):
         tt(D["wa"], D["w0"], D["RG"], ALU.is_gt)
         mm([(D["pf"], [(M128("TrS"), D["wa"])])])
         tt(D["am"], D["wa"], D["pf"], ALU.is_gt)
-        tt(D["t2"], D["am"], D["CmH"], ALU.mult)
-        tt(D["De"], D["t1"], D["t2"], ALU.add)
+        tt(D["cp"], D["am"], D["CmH"], ALU.mult)
+        tt(D["De"], D["t1"], D["cp"], ALU.add)
         tt(D["chf"], D["De"], D["Hr"], ALU.add)
         cp(D["chu"], D["chf"])
-        mm([(D["Vp"], [(In, V(D["h"][0], b, e, 16)) for b in range(16)])], (True, False))
         for a, b in cut(n, PC):
             act(sub(D["ch"], a, b, 16), ind(X, sub(D["chu"], a, b)), ACT.Copy)
 
@@ -473,7 +489,6 @@ def rank_program(g, core, T, topo):
         cp(D["p2"], D["up"])
         ts(D["p2"], D["p2"], 4095, ALU.bitwise_and)
         tt(D["p2"], D["p2"], D["HS"], ALU.mult)
-        ts(D["p2"], D["p2"], 5, ALU.arith_shift_right)
 
     def scat(t, o, n):
         phase("sc", o)
@@ -483,6 +498,7 @@ def rank_program(g, core, T, topo):
         D = names(t, j)
         n, e, o = D["n"], D["e"], D["o"]
         phase("vo", j)
+        mm([(D["Vp"], [(In, V(D["h"][0], b, e, 16)) for b in range(16)])], (True, False))
         mm([(D["Vp"], [(I1, V(D["ch"][0], b, e, 16)) for b in range(16)])], (False, True))
         act(D["sg"], D["Vp"], ACT.Sign, bias=0.5)
         GB = M128("GBb")
@@ -503,10 +519,8 @@ def rank_program(g, core, T, topo):
             mm([(D["bp"], [(M128("Tr1"), D["sp"])])])
             tt(D["r"], D["sp"], D["bp"], ALU.mult)
             ts(D["r"], D["r"], 1, ALU.bitwise_and)
-            tt(D["sOp"], D["r"], D["CmH"], ALU.mult)
+            tt(D["sO"], D["r"], D["CmH"], ALU.mult)
             tt(D["sOm"], D["sp"], D["OmH"], ALU.mult)
-            tt(D["jd"], D["jd"], D["sOp"], ALU.add)
-            tt(D["ym"], D["sOp"], D["sOm"], ALU.subtract)
 
     def post(t, j):
         D = names(t, j)
@@ -515,16 +529,17 @@ def rank_program(g, core, T, topo):
         phase("po", j)
         on = V("on16", 0, n)
         L = [(H1, D["Hc"]), (F1, D["jd"])]
-        L2 = [(H1, D["Oc"]), (M128("H2048"), on)]
+        L2 = [(M128("H32"), D["Oc"]), (M128("H2048"), V("m96", 0, n))]
         if t:
-            L2 += [(M128("HK"), D["stl"]), (F1, D["ym"])]
+            L += [(F1, D["sO"])]
+            L2 += [(M128("HK"), D["stl"]), (M128("HK"), D["stl"]), (M128("F32"), D["sO"]), (M128("F32n"), D["sOm"])]
         mm([(D["H2"], L), (D["S2"], L2)])
         if t < READS - 1:
             ts(D["Hs"], D["H2"], 2048.0, ALU.add)
         else:
             ts(V("oyb", o, o + n), D["H2"], 2048.0, ALU.add)
         tt(D["p2"], D["p2"], D["S2"], ALU.add)
-        ts(D["p2"], D["p2"], 4095, ALU.bitwise_and)
+        ts(D["p2"], D["p2"], 5, ALU.arith_shift_right, 4095, ALU.bitwise_and)
         if t < READS - 1:
             cp(D["Os"], D["p2"])
             su, sz = "su%d" % t, "sz%d" % t
@@ -548,7 +563,7 @@ def rank_program(g, core, T, topo):
         b = 8 * (t % 2)
         kb = "p%d" % (2 + (t * NCH + NCH - 1) % 2)
         mm([(V(kb, 500, 501), [(M128("FK"), V("kacc", b + j, b + j + 1)) for j in range(NCH)])])
-        ts(V("kcol", 0, 1), V(kb, 500, 501), 1024.0, ALU.add)
+        ts(V("kcol", 0, 1), V(kb, 500, 501), 16384.0, ALU.add)
         ts(M128("HK"), M128("H1"), V("kcol", 0, 1), ALU.mult)
 
     pre(0, 0)

from concourse.mybir import dt, AluOpType as ALU, ActivationFunctionType as ACT

CH = [96, 96, 64]
NCH = len(CH)
OFF = [sum(CH[:j]) for j in range(NCH)]
NM = max(CH)
NB = 3
READS = 4
NENG = 8
RELU = [(), (), ()]
PH, PD, PC, DHV = 48, 48, 48, True

SCRATCH = {
    "X": ("sbuf", [128, 4096], "bfloat16"),
    "li": ("sbuf", [128, 512], "int32"),
    "wcol": ("sbuf", [128, 1], "bfloat16"),
    "Eb": ("sbuf", [128, 144], "bfloat16"), "Ew": ("sbuf", [128, 144], "bfloat16"),
    "GBb": ("sbuf", [128, 128], "bfloat16"), "Ib": ("sbuf", [128, 128], "bfloat16"),
    "Ibn": ("sbuf", [128, 128], "bfloat16"), "Ib128": ("sbuf", [128, 128], "bfloat16"),
    "Ibh": ("sbuf", [128, 128], "bfloat16"), "TrS": ("sbuf", [128, 128], "bfloat16"),
    "Tr1": ("sbuf", [128, 128], "bfloat16"), "ones": ("sbuf", [128, 144], "bfloat16"),
    "tmpw": ("sbuf", [128, 144], "bfloat16"), "tmpw2": ("sbuf", [128, 144], "bfloat16"),
    "tmpt": ("sbuf", [128, 128], "bfloat16"),
    "H1": ("sbuf", [128, 128], "float16"), "Hn": ("sbuf", [128, 128], "float16"),
    "H2080": ("sbuf", [128, 128], "float16"), "H3232": ("sbuf", [128, 128], "float16"),
    "H32": ("sbuf", [128, 128], "float16"), "m96": ("sbuf", [128, NM], "float16"),
    "F32": ("sbuf", [128, 128], "float32"), "F32n": ("sbuf", [128, 128], "float32"),
    "H2048": ("sbuf", [128, 128], "float16"), "H256": ("sbuf", [128, 128], "float16"),
    "HK": ("sbuf", [128, 128], "float16"), "on16": ("sbuf", [128, NM], "float16"),
    "F1": ("sbuf", [128, 128], "float32"), "FK": ("sbuf", [128, 128], "float32"),
    "E2": ("sbuf", [128, 144], "bfloat16"), "En": ("sbuf", [128, 144], "bfloat16"),
    "Wb": ("sbuf", [128, 128], "bfloat16"),
    "bi": ("sbuf", [128, 32], "int32"), "base": ("sbuf", [128, 16], "int32"),
    "RST": ("sbuf", [128, 16 * NM], "bfloat16"),
    "kacc": ("sbuf", [128, 16], "float32"), "kcol": ("sbuf", [128, 1], "float32"),
    "junk": ("sbuf", [128, NM], "bfloat16"),
    "ul": ("sbuf", [128, 32], "int32"),
    "nl": ("sbuf", [128, 32], "uint16"), "xv": ("sbuf", [128, 256], "int32"),
    "oya": ("sbuf", [128, 256], "float32"), "oyb": ("sbuf", [128, 256], "float32"),
    "oyi": ("sbuf", [128, 256], "float32"), "oyg": ("sbuf", [128, 256], "float32"),
}
for _t in range(READS):
    SCRATCH["lu%d" % _t] = ("sbuf", [128, 512], "uint16")
    SCRATCH["mz%d" % _t] = ("sbuf", [128, 768], "bfloat16")
    if _t < READS - 1:
        SCRATCH["su%d" % _t] = ("sbuf", [128, 512], "uint16")
        SCRATCH["sz%d" % _t] = ("sbuf", [128, 768], "bfloat16")
for _p in range(2):
    SCRATCH["zs%d" % _p] = ("sbuf", [128, 16 * NM], "bfloat16")
for _p in range(NB):
    for _n in ("zr", "h", "do", "dc", "ah", "ao", "ac", "ch", "rm"):
        SCRATCH["%s%d" % (_n, _p)] = ("sbuf", [128, 16 * NM], "bfloat16")
    SCRATCH["f%d" % _p] = ("sbuf", [128, 8 * NM], "float32")
    SCRATCH["b%d" % _p] = ("sbuf", [128, 9 * NM], "bfloat16")
    SCRATCH["s%d" % _p] = ("sbuf", [128, 4 * NM], "float16")
    SCRATCH["i%d" % _p] = ("sbuf", [128, 3 * NM], "int32")
    SCRATCH["u%d" % _p] = ("sbuf", [128, 2 * NM], "uint16")
for _p in range(8):
    SCRATCH["p%d" % _p] = ("psum", [128, 512], "float32")

SEMAPHORES = ["qv", "qt", "qa", "qg", "left"]
SEMAPHORES += ["x%d" % k for k in range(4)] + ["la%d" % k for k in range(NCH)] + ["lz", "lw"]
SEMAPHORES += ["rl%d_%d" % (t, j) for t in range(1, READS) for j in range(NCH)]
SEMAPHORES += ["rz%d_%d" % (t, j) for t in range(1, READS) for j in range(NCH)]
SEMAPHORES += ["out%d" % k for k in range(4 * NCH)]

EST = {"cy": 1.0, "gam": 1.56, "scat": 3.0, "pec": 0.5, "fv": 0.0, "fa": 0.0, "ft": 0.0, "wake": 80.0, "net": 6500.0, "dma": 2000.0, "iss": 500.0}
SHIFT = {'s12': '5:-56 16:123 13:-23 3:-20 8:-37 9:102 14:-23 2:-20 x:-8 6:25 4:4 15:20', 's11': '9:-22 12:208 10:-58 18:36 14:-14 6:-7 13:-23 1:-35 7:12 17:45 0:-12 5:-8 11:12 16:-1 x:-1 15:19 8:-24', 'ch2': '2:-22 13:111 x:-159 12:57 5:-37 0:-40 4:-12 1:-8 11:76 8:17 14:15 3:-53 9:-5', 'vo0': '10:-47 11:139 13:-44 2:69 8:39 12:43 0:-144 15:-6 3:5 9:9 6:20 5:6 7:1 x:1 1:33', 'vo2': '1:40 10:129 14:-103 0:93 8:-32 11:-46 12:16 3:98 15:-43 2:6 5:4 13:-5 7:15 6:-5 9:-7 4:-27', 'ch1': 'x:1 12:5 1:115 0:38 13:-66 6:-51 14:16 5:-35 9:-31 8:-12 4:15 7:17 3:36 11:7', 'ch0': '13:22 14:1 1:84 0:1 6:16 12:213 8:72 x:9 4:39 3:-7 7:16 9:-2', 'c': '19:24 5:22 27:51 26:-14 40:23 37:128 43:22 1:-71 39:94 9:-65 25:-18 4:55 38:-36 30:22 33:-73 42:-17 29:-154 10:60 12:80 23:-11 2:132 0:-95 17:-13 11:11 41:1 7:-21 49:20 6:32 15:19 14:4 48:35 28:1 45:-15 20:36 3:-24 44:-8 8:29 18:-13 22:-26', 'kc0': '2:-2 1:-8 x:-286 0:-23', 'pre0': '13:-16 12:48 5:-12 3:128 8:-3 10:-34 1:-44 x:-1 0:-29', 'pre2': '7:-64 12:-19 2:-21 8:-43 6:-2 1:27 0:-22 x:-4 10:-14 3:-12 13:-8', 'up2': '7:29 6:-8 x:24 8:-33 1:-21 9:-150 0:-12 10:-75 12:-11 3:15 4:26 14:10 5:-7', 'up1': '10:4 14:-122 x:101 1:164 4:-110 6:-25 12:46 11:2 9:-36 3:-6 8:-11 0:5 2:33', 'up0': '14:-82 9:10 2:28 5:-45 8:-91 0:-6 6:-132 13:25 3:-29 11:107 12:-7', 'po0': '6:-12 0:54 8:-23 5:-10 7:57 4:40 9:-38 10:54 3:35 x:14', 'pre1': '1:-16 7:4 4:4 5:71 12:42 9:1 3:1 11:-1 0:-15', 'vo1': '15:-72 x:54 11:-15 13:20 12:-52 14:-37 8:-43 9:132 4:-102 0:-55 10:-24 7:12 6:-35 1:-32 2:-52 5:51 3:19', 'po1': '0:33 9:63 7:23 1:12 5:-78 3:-3 x:3 4:-24 8:-6 10:-46 2:16', 's10': '5:118 0:110 13:40 3:-30 2:-12 12:-15 16:62 11:-7 15:-7 9:3 17:-35 6:-99 7:4 14:59', 'po2': '5:11 2:-4 7:25 10:-50 6:-55 x:29 4:41 9:11 1:-16 3:22 8:74 0:2', 'sc192': '0:88 x:4', 'sc0': '0:-11 x:-10'}
BONUS = {}
for _p, _s in SHIFT.items():
    for _e in _s.split():
        _i, _v = _e.split(":")
        BONUS[_p if _i == "x" else _p + ":" + _i] = 100.0 * int(_v)


def price(w, E):
    k, n = w[0], w[1]
    if k == "v":
        return E["fv"] + E["cy"] * max(64.0, n)
    if k == "vg":
        return 50.0 + E["cy"] * E["gam"] * n
    if k == "vs":
        return 50.0 + E["cy"] * E["scat"] * n
    if k == "a":
        return E["fa"] + E["cy"] * n
    if k == "ag":
        return 65.0 + E["cy"] * E["gam"] * n
    if k == "t":
        return E["pec"] * n + E["ft"] * w[2]
    return E[k] if k in E else n


def cv(n, f=1.0):
    return ("v", n * f)


def ca(n, f=1.0):
    return ("a", n) if f == 1.0 else ("ag", n)


def schedule(ops, E, bonus):
    N = len(ops)
    W = E["wake"]
    cost = [price(o["w"], E) for o in ops]
    succ = [[] for _ in range(N)]
    for k in range(N):
        for d in ops[k]["deps"]:
            succ[d].append(k)
    bot = [0.0] * N
    for k in range(N - 1, -1, -1):
        bot[k] = cost[k] + W + max([bot[s] for s in succ[k]] + [0.0])
    pri = [bot[k] + bonus.get(ops[k]["tag"], 0.0) + bonus.get(ops[k]["tag"].split(":")[0], 0.0) for k in range(N)]
    left = [len(o["deps"]) for o in ops]
    ready, free, order = {}, {}, []
    rt, fin = [0.0] * N, [0.0] * N
    for k in range(N):
        ready.setdefault(ops[k]["q"], [])
        if left[k] == 0:
            ready[ops[k]["q"]].append(k)
    while len(order) < N:
        best = None
        for q, lst in ready.items():
            if not lst:
                continue
            f = 0.0 if q == "n" else free.get(q, 0.0)
            st = max(f, min([rt[k] for k in lst]))
            if best is None or st < best[0]:
                best = (st, q, lst)
        st, q, lst = best
        k = max([k for k in lst if rt[k] <= st + 1e-9], key=lambda k: pri[k])
        lst.remove(k)
        dma = q in ("s", "s2")
        free[q] = st + (60.0 if dma else cost[k])
        fin[k] = st + cost[k]
        order.append(k)
        for s in succ[k]:
            left[s] -= 1
            rt[s] = max(rt[s], fin[k] + (W if ops[s]["deps"][k] else 0.0))
            if left[s] == 0:
                ready[ops[s]["q"]].append(s)
    return order, fin


def rank_program(g, core, T, topo):
    rank = T.rank_of(core)
    if rank is None:
        return
    ops = []
    hist = {}
    cur = ["c", 0]

    def phase(name, j):
        cur[0], cur[1] = "%s%d" % (name, j), 0

    def R(name, a, b):
        return (name, a, b)

    def add(q, fn, rd, wr, cost, sem=None, inc=1, after=()):
        k = len(ops)
        deps = {}
        for isw, regs in ((False, rd), (True, wr)):
            for (nm, a, b) in regs:
                bank = nm[0] == "p" and nm[1:].isdigit()
                for (d, da, db, dw) in hist.get(nm, ()):
                    same = ops[d]["q"] == q
                    over = a < db and da < b
                    if bank and not same:
                        deps[d] = True
                    elif over and (isw or dw):
                        deps[d] = deps.get(d, False) or dw or not same
        for d in after:
            deps[d] = True
        for isw, regs in ((False, rd), (True, wr)):
            for (nm, a, b) in regs:
                lst = hist.setdefault(nm, [])
                if isw:
                    bank = nm[0] == "p" and nm[1:].isdigit()
                    if not bank:
                        lst = [e for e in lst if not (a <= e[1] and e[2] <= b)]
                    else:
                        lst = lst[-24:]
                    hist[nm] = lst
                lst.append((k, a, b, isw))
        deps.pop(k, None)
        w = ("dma", 0) if q in ("s", "s2") else cost if isinstance(cost, tuple) else ("x", cost)
        ops.append({"q": q, "fn": fn, "deps": deps, "w": w, "sem": sem, "inc": inc, "tag": "%s:%d" % (cur[0], cur[1])})
        cur[1] += 1
        return k

    def V(name, a, b, step=1):
        return (name, a, b, step)

    def ap(v):
        if len(v) == 5:
            o = v[4]
            return T[v[0]][:, v[1]:v[2]].indirect(T[o[0]][:, o[1]:o[2]])
        if v[3] == 1:
            return T[v[0]][:, v[1]:v[2]]
        return T[v[0]][:, v[1]:v[2]:v[3]]

    def ind(win, off):
        return (win[0], win[1], win[2], 1, off)

    def regs(*vs):
        r = []
        for v in vs:
            r.append((v[0], v[1], v[2]))
            if len(v) == 5:
                r.append((v[4][0], v[4][1], v[4][2]))
        return r

    def cnt(v):
        if len(v) == 5:
            return 16 * (v[4][2] - v[4][1])
        return (v[2] - v[1] + v[3] - 1) // v[3]

    two = ("bfloat16", "uint16", "float16")

    def half(*vs):
        return 0.5 if all(SCRATCH[v[0]][2] in two for v in vs) else 1.0

    def tt(out, in0, in1, op):
        n = cnt(out) if len(out) < 5 else cnt(in0)
        if len(in0) == 5:
            c = ("vg", n)
        else:
            c = cv(n, 1.0 if (in0[0][0] == "p" or in1[0][0] == "p") else 2.0)
        return add("v", lambda: g.vector.tensor_tensor(ap(out), ap(in0), ap(in1), op), regs(in0, in1), regs(out), c)

    def ts(out, in0, s1, op0, s2=None, op1=None):
        rd = regs(in0) + [(s[0], s[1], s[2]) for s in (s1, s2) if isinstance(s, tuple)]

        def emit():
            a1 = ap(s1) if isinstance(s1, tuple) else s1
            a2 = ap(s2) if isinstance(s2, tuple) else s2
            if op1 is None:
                return g.vector.tensor_scalar(ap(out), ap(in0), a1, None, op0)
            return g.vector.tensor_scalar(ap(out), ap(in0), a1, a2, op0, op1)
        return add("v", emit, rd, regs(out), cv(cnt(in0), half(out, in0)))

    def cp(out, in_):
        if len(out) == 5:
            c = ("vs", cnt(in_))
            return add("v", lambda: g.vector.tensor_copy(ap(out), ap(in_)), regs(in_) + [(out[4][0], out[4][1], out[4][2])], [(out[0], out[1], out[2])], c)
        return add("v", lambda: g.vector.tensor_copy(ap(out), ap(in_)), regs(in_), regs(out), cv(cnt(in_), half(out, in_)))

    def scan(out, d0, d1, o0, o1):
        return add("v", lambda: g.vector.tensor_tensor_scan(ap(out), ap(d0), ap(d1), 0.0, o0, o1), regs(d0, d1), regs(out), cv(cnt(out), 0.5))

    def fill(out, c):
        return add("v", lambda: g.vector.memset(ap(out), c), [], regs(out), cv(cnt(out), half(out)))

    def act(out, in_, func, bias=0.0, scale=1.0, acc=None):
        n = cnt(out)
        c = ca(n, 2.0 if len(in_) == 5 else 1.0)
        wr = regs(out) + (regs(acc) if acc is not None else [])

        def emit():
            if acc is not None:
                return g.scalar.activation(ap(out), ap(in_), func, bias=bias, scale=scale, accum_out=ap(acc))
            return g.scalar.activation(ap(out), ap(in_), func, bias=bias, scale=scale)
        return add("a", emit, regs(in_), wr, c)

    def mm(groups, part=(True, True)):
        first, final = part
        rd, wr, c, m = [], [], 0.0, 0
        for out, lst in groups:
            wr += regs(out)
            for l, r in lst:
                rd += regs(l, r)
                m += 1
                c += max(64, cnt(r)) * (4 if SCRATCH[r[0]][2] == "float32" else 1)

        def emit():
            last = None
            for out, lst in groups:
                for k, (l, r) in enumerate(lst):
                    last = g.tensor.matmul(ap(out), ap(l), ap(r), first and k == 0, final and k == len(lst) - 1)
            return last
        return add("t", emit, sorted(set(rd)), wr, ("t", c, m))

    def gp(fn, rd, wr, c):
        return add("g", fn, regs(*rd), regs(*wr), c)

    def M128(name):
        return V(name, 0, 128)

    for k in range(4):
        a, b = 1024 * k, 1024 * (k + 1)
        add("s" if k % 2 else "s2", (lambda a=a, b=b, k=k: (g.sync if k % 2 else g.scalar).dma_start(T.X[:, a:b], T.xt[:, a:b])), [], [R("X", a, b)], 1500.0, "x%d" % k, 16)
    for j in range(NCH):
        o, n = OFF[j], CH[j]
        add("s", (lambda o=o, n=n: g.sync.dma_start(T.li[:, 2 * o:2 * o + n], T.ba[:, o:o + n])), [], [R("li", 2 * o, 2 * o + n)], 1500.0, "la%d" % j, 16)
        add("s", (lambda o=o, n=n: g.sync.dma_start(T.li[:, 2 * o + n:2 * o + 2 * n], T.bb[:, o:o + n])), [], [R("li", 2 * o + n, 2 * o + 2 * n)], 1500.0, "la%d" % j, 16)
        add("s", (lambda o=o, n=n: g.sync.dma_start(T.mz0[:, 3 * o:3 * o + n], T.zp[:, o:o + n])), [], [R("mz0", 3 * o, 3 * o + n)], 1500.0, "la%d" % j, 16)
    add("s", lambda: g.sync.dma_start(T.wcol[:], T.wl[:]), [], [R("wcol", 0, 1)], 1500.0, "lw", 16)
    for k in ops:
        if k["sem"] is not None and k["sem"].startswith("la"):
            k["need"] = 48

    fill(V("ones", 0, 144), 1.0)
    gp(lambda: g.iota(T.bi[:, 0:16], [[0, 16]], 0, 16), [], [V("bi", 0, 16)], 200.0)
    gp(lambda: g.iota(T.bi[:, 16:32], [[256, 16]], 0, 0), [], [V("bi", 16, 32)], 200.0)
    W9 = V("ones", 0, 144)
    gp(lambda: g.affine_select(T.tmpw[:], T.ones[:], [[-16, 9], [0, 16]], ALU.is_ge, 0.0, 0, 1), [W9], [V("tmpw", 0, 144)], 450.0)
    gp(lambda: g.affine_select(T.tmpw2[:], T.tmpw[:], [[16, 9], [0, 16]], ALU.is_ge, 0.0, 15, -1), [V("tmpw", 0, 144)], [V("tmpw2", 0, 144)], 450.0)
    cp(M128("GBb"), V("tmpw2", 0, 128))
    gp(lambda: g.affine_select(T.Ib[:], T.GBb[:], [[1, 128]], ALU.is_equal, 0.0, 0, -1), [M128("GBb")], [M128("Ib")], 450.0)
    gp(lambda: g.affine_select(T.Eb[:], T.tmpw2[:], [[0, 9], [1, 16]], ALU.is_equal, 0.0, -15, 0), [V("tmpw2", 0, 144)], [V("Eb", 0, 144)], 450.0)
    gp(lambda: g.affine_select(T.Tr1[:], T.GBb[:], [[1, 128]], ALU.is_ge, 0.0, -1, -1), [M128("GBb")], [M128("Tr1")], 450.0)
    for nm, c in (("H1", 1.0), ("Hn", -1.0), ("H2080", 2080.0), ("H3232", 3232.0), ("H32", 32.0), ("F32", 32.0), ("F32n", -32.0), ("H2048", 2048.0), ("Ibn", -1.0), ("Ib128", 128.0), ("Ibh", 0.5), ("H256", 256.0), ("F1", 1.0)):
        ts(M128(nm), M128("Ib"), c, ALU.mult)
    ts(M128("TrS"), M128("Tr1"), 0.21875, ALU.mult)
    cp(V("on16", 0, NM), V("ones", 0, NM))
    ts(V("m96", 0, NM), V("ones", 0, NM), -96.0, ALU.mult)
    fill(V("RST", 0, 16 * NM), 1.0)
    add("v", lambda: g.vector.memset(T.RST[:, 0:16 * NM:16], 0.0), [], [R("RST", 0, 16 * NM)], cv(NM))
    for p in range(2):
        act(V("zs%d" % p, 0, 16 * NM), V("RST", 0, 16 * NM), ACT.Copy, scale=0.0)
    ts(V("Ew", 0, 144), V("Eb", 0, 144), V("wcol", 0, 1), ALU.mult)
    ts(V("E2", 0, 144), V("Eb", 0, 144), 2.0, ALU.mult)
    ts(V("En", 0, 144), V("Eb", 0, 144), -1.0, ALU.mult)
    fill(M128("FK"), -0.5)
    ts(M128("Wb"), M128("GBb"), V("wcol", 0, 1), ALU.mult)
    ts(V("bi", 0, 16), V("bi", 0, 16), 255, ALU.bitwise_and)
    tt(V("base", 0, 16), V("bi", 0, 16), V("bi", 16, 32), ALU.add)

    def E(b, nm="Eb"):
        return V(nm, 15 - b, 15 - b + 128)

    nxt, prv = T.cores[(rank + 1) % len(T.cores)], T.cores[(rank - 1) % len(T.cores)]
    sends = {}
    X = V("X", 0, 4096)

    def names(t, j):
        q = t * NCH + j
        p, o, n = q % NB, OFF[j], CH[j]
        e = 16 * n
        D = {"q": q, "p": p, "o": o, "n": n, "e": e}
        for nm in ("zr", "h", "do", "dc", "ah", "ao", "ac", "ch", "rm"):
            D[nm] = V("%s%d" % (nm, p), 0, e)

        def slot(base, k, w=None):
            return V("%s%d" % (base, p), k * NM, k * NM + (w or n))
        for k, nm in enumerate(("dhs", "m1", "t1", "De", "jd", "sOm", "sO", "chf")):
            D[nm] = slot("f", k)
        for k, nm in enumerate(("rec", "w0", "wa", "am", "sg", "J", "sp", "nIo", "Gno")):
            D[nm] = slot("b", k)
        D["HO"] = V("s%d" % p, 0, 2 * n)
        D["Hc"], D["Oc"] = V("s%d" % p, 0, n), V("s%d" % p, n, 2 * n)
        D["stl"], D["Cc"] = slot("s", 2), slot("s", 3)
        D["pm"], D["r"], D["p2"] = slot("i", 0), slot("i", 1), slot("i", 2)
        D["Cu"], D["chu"] = slot("u", 0), slot("u", 1)
        lu, mz = "lu%d" % t, "mz%d" % t
        D["LU"] = V(lu, 2 * o, 2 * o + 2 * n)
        D["Hu"], D["Ou"] = V(lu, 2 * o, 2 * o + n), V(lu, 2 * o + n, 2 * o + 2 * n)
        D["z"], D["nI"], D["G"] = [V(mz, 3 * o + k * n, 3 * o + (k + 1) * n) for k in range(3)]
        if t < READS - 1:
            su, sz = "su%d" % t, "sz%d" % t
            D["Hs"], D["Os"] = V(su, 2 * o + n, 2 * o + 2 * n), V(su, 2 * o, 2 * o + n)
            D["zn"], D["nIn"], D["Gn"] = [V(sz, 3 * o + k * n, 3 * o + (k + 1) * n) for k in range(3)]
            if t == 0:
                D["J"] = D["nIn"]
        else:
            D["nIn"] = D["nIo"]
            D["Gn"] = D["Gno"]

        def ps(bk, k):
            return V("p%d" % bk, k * n, k * n + n)
        lb, db = 4 + q % 3, 2 + q % 2
        for nm, k in (("OmH", 0), ("CmH", 1), ("Op", 2), ("HS", 2), ("S", 3), ("Y", 3), ("bp", 3), ("Hr", 4)):
            D[nm] = ps(lb, k)
        for nm, k in (("dh", 0), ("ddo", 1), ("ddc", 2), ("RG", 3), ("pf", 4), ("cp", 1), ("up", 2), ("zM", 3)):
            D[nm] = ps(db, k)
        D["UL"] = V("p%d" % db, 480, 480 + n // 16)
        for nm, k in (("Vp", 0), ("X1", 1), ("X2", 2), ("sc", 3), ("H2", 3), ("S2", 4)):
            D[nm] = ps(7, k)
        return D

    I1, In, F1 = M128("Ib"), M128("Ibn"), M128("F1")
    H1, Hn = M128("H1"), M128("Hn")

    def cut(n, w):
        m = max(1, (n + w - 1) // w)
        s = [2 * (n // 2 * i // m) for i in range(m + 1)]
        return list(zip(s[:-1], s[1:]))

    def sub(v, a, b, k=1):
        return V(v[0], v[1] + k * a, v[1] + k * b)

    def pre(t, j):
        phase("pre", j)
        D = names(t, j)
        n = D["n"]
        if t == 0:
            li = V("li", 2 * D["o"], 2 * D["o"] + 2 * n)
            cp(D["LU"], li)
            ts(D["HO"], li, -2048.0, ALU.add)
        else:
            for nm, v in (("rl", D["LU"]), ("rz", V(D["z"][0], 3 * D["o"], 3 * D["o"] + 3 * n))):
                k = add("n", None, [], regs(v), ("net", 0), "%s%d_%d" % (nm, t, j), NENG, after=[sends[(nm, t - 1, j)]])
                ops[k]["soft"] = True
            ts(D["HO"], D["LU"], -2048.0, ALU.add)
        on = V("on16", 0, n)
        mm([(D["Op"], [(H1, D["Oc"])]), (D["S"], [(M128("H2080"), D["Hc"]), (M128("H3232"), D["Oc"])]),
            (D["OmH"], [(H1, D["Oc"]), (Hn, D["Hc"])]), (D["Hr"], [(H1, D["Hc"]), (M128("H2048"), on)])])
        tt(D["pm"], D["Hc"], D["Op"], ALU.mult)
        tt(D["pm"], D["pm"], D["S"], ALU.add)
        ts(D["pm"], D["pm"], 5, ALU.arith_shift_right, 4095, ALU.bitwise_and)
        cp(D["Cu"], D["pm"])
        ts(D["stl"], D["OmH"], 0.0, ALU.is_equal)
        tt(D["HS"], D["stl"], D["Hr"], ALU.mult)
        tt(D["CmH"], D["pm"], D["Hr"], ALU.subtract)
        zs = "zs%d" % (D["q"] % 2)
        add("v", lambda: g.vector.tensor_copy(T[zs][:, 0:D["e"]:16], ap(D["z"])), regs(D["z"]), [R(zs, 0, D["e"])], cv(n, 0.5))
        for a in range(0, D["e"], 512):
            scan(V(D["zr"][0], a, a + 512), V("RST", a, a + 512), V(zs, a, a + 512), ALU.mult, ALU.add)

    def s1(t, j):
        D = names(t, j)
        n, e = D["n"], D["e"]
        phase("s1", j)
        for a, b in cut(n, PH):
            act(sub(D["h"], a, b, 16), ind(X, sub(D["Hu"], a, b)), ACT.Copy)
        for dst, lst in (("do", "Ou"), ("dc", "Cu")):
            for a, b in cut(n, PD):
                tt(sub(D[dst], a, b, 16), ind(X, sub(D[lst], a, b)), sub(D["zr"], a, b, 16), ALU.subtract)
        for k in range(n // 32):
            a, b = 512 * k, 512 * k + 512
            bk = V("p%d" % (k % 2), 0, 512)
            mm([(bk, [(I1, V(D["h"][0], a, b)), (In, V(D["zr"][0], a, b))])])
            act(V(D["ah"][0], a, b), bk, ACT.Abs)
        for src, dst in (("do", "ao"), ("dc", "ac")):
            for a, b in cut(n, PD):
                if src in RELU[j]:
                    ts(sub(D[dst], a, b, 16), sub(D[src], a, b, 16), 0.0, ALU.max)
                else:
                    act(sub(D[dst], a, b, 16), sub(D[src], a, b, 16), ACT.Abs)
        for raw, src, dst in ((None, "ah", "dh"), ("do", "ao", "ddo"), ("dc", "ac", "ddc")):
            if raw in RELU[j]:
                mm([(D[dst], [(E(b, "En"), V(D[raw][0], b, e, 16)) for b in range(16)] +
                     [(E(b, "E2"), V(D[src][0], b, e, 16)) for b in range(16)])])
            else:
                mm([(D[dst], [(E(b), V(D[src][0], b, e, 16)) for b in range(16)])])

    def choice(t, j):
        D = names(t, j)
        n, e = D["n"], D["e"]
        phase("ch", j)
        cp(D["dhs"], D["dh"]) if DHV else act(D["dhs"], D["dh"], ACT.Copy)
        tt(D["m1"], D["dhs"], D["ddc"], ALU.min)
        tt(D["rec"], D["m1"], D["ddo"], ALU.is_ge)
        tt(D["w0"], D["dhs"], D["ddc"], ALU.is_gt)
        hb = M128("Ibh")
        mm([(D["RG"], [(H1, D["stl"])] + ([(hb, D["G"]), (hb, V("ones", 0, n))] if t else []) + [(I1, D["rec"])])])
        tt(D["t1"], D["rec"], D["OmH"], ALU.mult)
        tt(D["wa"], D["w0"], D["RG"], ALU.is_gt)
        mm([(D["pf"], [(M128("TrS"), D["wa"])])])
        tt(D["am"], D["wa"], D["pf"], ALU.is_gt)
        tt(D["cp"], D["am"], D["CmH"], ALU.mult)
        tt(D["De"], D["t1"], D["cp"], ALU.add)
        tt(D["chf"], D["De"], D["Hr"], ALU.add)
        cp(D["chu"], D["chf"])
        for a, b in cut(n, PC):
            act(sub(D["ch"], a, b, 16), ind(X, sub(D["chu"], a, b)), ACT.Copy)

    def upd(t, j):
        D = names(t, j)
        n, e, o = D["n"], D["e"], D["o"]
        phase("up", j)
        for a, b in cut(n, PC):
            scan(sub(D["rm"], a, b, 16), V("RST", 16 * a, 16 * b), sub(D["ch"], a, b, 16), ALU.mult, ALU.max)
        k = n // 16
        c0 = o // 16
        U0, U1 = V("ul", c0, c0 + k), V("ul", 16 + c0, 16 + c0 + k)
        nl = V("nl", c0, c0 + k)
        if t < READS - 1:
            mm([(D["UL"], [(E(r, "Ew"), V(D["rm"][0], 16 * r + 15, e, 256)) for r in range(16)])])
            cp(U0, D["UL"])
            ts(U1, U0, 15, ALU.bitwise_and)
            tt(U1, U1, V("base", c0, c0 + k), ALU.add)
            cp(nl, U1)
            xv = V("xv", o, o + n)
            tt(xv, ind(X, nl), V(D["rm"][0], 15, e, 16), ALU.add)
            ts(xv, xv, 1, ALU.arith_shift_right)
            mm([(D["zM"], [(I1, D["z"]), (In, V(D["rm"][0], 15, e, 16))])])
            act(D["zn"], D["zM"], ACT.Abs)
        mm([(D["up"], [(M128("Wb"), V(D["rm"][0], 15, e, 16))])])
        cp(D["p2"], D["up"])
        ts(D["p2"], D["p2"], 4095, ALU.bitwise_and)
        tt(D["p2"], D["p2"], D["HS"], ALU.mult)

    def scat(t, o, n):
        phase("sc", o)
        cp(ind(X, V("nl", o // 16, (o + n) // 16)), V("xv", o, o + n))

    def vote(t, j):
        D = names(t, j)
        n, e, o = D["n"], D["e"], D["o"]
        phase("vo", j)
        mm([(D["Vp"], [(In, V(D["h"][0], b, e, 16)) for b in range(16)])], (True, False))
        mm([(D["Vp"], [(I1, V(D["ch"][0], b, e, 16)) for b in range(16)])], (False, True))
        act(D["sg"], D["Vp"], ACT.Sign, bias=0.5)
        GB = M128("GBb")
        gr = [(D["X1"], [(GB, D["sg"]), (M128("Ib128"), D["rec"]), (M128("Ib128"), D["am"]), (M128("H256"), D["stl"])]),
              (D["X2"], [(GB, D["sg"]), (M128("Ib128"), D["am"])] + ([(M128("Ib128"), D["G"])] if t else []))]
        if t < READS - 1:
            gr.append((D["sc"], [(GB, D["sg"])]))
        mm(gr)
        ts(D["J"], D["X1"], 126.0, ALU.is_ge)
        act(D["Gn"], D["X2"], ACT.Sign, bias=3.0 if t else -125.0)
        if t < READS - 1:
            act(V("junk", 0, n), D["sc"], ACT.Sign, bias=3.0, acc=V("kacc", 8 * (t % 2) + j, 8 * (t % 2) + j + 1))
        tt(D["jd"], D["J"], D["De"], ALU.mult)
        if t:
            mm([(D["Y"], [(I1, D["nI"]), (I1, D["J"])])])
            act(D["sp"], D["Y"], ACT.Relu, bias=1.0, scale=-1.0)
            act(D["nIn"], D["Y"], ACT.Square, bias=1.0, scale=-1.0)
            mm([(D["bp"], [(M128("Tr1"), D["sp"])])])
            tt(D["r"], D["sp"], D["bp"], ALU.mult)
            ts(D["r"], D["r"], 1, ALU.bitwise_and)
            tt(D["sO"], D["r"], D["CmH"], ALU.mult)
            tt(D["sOm"], D["sp"], D["OmH"], ALU.mult)

    def post(t, j):
        D = names(t, j)
        n, e, o = D["n"], D["e"], D["o"]
        k, c0 = n // 16, o // 16
        phase("po", j)
        on = V("on16", 0, n)
        L = [(H1, D["Hc"]), (F1, D["jd"])]
        L2 = [(M128("H32"), D["Oc"]), (M128("H2048"), V("m96", 0, n))]
        if t:
            L += [(F1, D["sO"])]
            L2 += [(M128("HK"), D["stl"]), (M128("HK"), D["stl"]), (M128("F32"), D["sO"]), (M128("F32n"), D["sOm"])]
        mm([(D["H2"], L), (D["S2"], L2)])
        if t < READS - 1:
            ts(D["Hs"], D["H2"], 2048.0, ALU.add)
        else:
            ts(V("oyb", o, o + n), D["H2"], 2048.0, ALU.add)
        tt(D["p2"], D["p2"], D["S2"], ALU.add)
        ts(D["p2"], D["p2"], 5, ALU.arith_shift_right, 4095, ALU.bitwise_and)
        if t < READS - 1:
            cp(D["Os"], D["p2"])
            su, sz = "su%d" % t, "sz%d" % t
            rid, pid = topo.addr(nxt, core)
            mask = sum(1 << x for x in topo.engines(core, nxt)[:NENG])
            lu, mz = "lu%d" % (t + 1), "mz%d" % (t + 1)

            def snd(src, dst, a, b, sem):
                return lambda: g.remote_dma(T[dst][:, a:b], T[src][:, a:b], T.sem[sem], T.sem.left, pid, rid, mask)
            sends[("rz", t, j)] = add("g", snd(sz, mz, 3 * o, 3 * o + 3 * n, "rz%d_%d" % (t + 1, j)), [R(sz, 3 * o, 3 * o + 3 * n)], [], 300.0, "left", NENG)
            sends[("rl", t, j)] = add("g", snd(su, lu, 2 * o, 2 * o + 2 * n, "rl%d_%d" % (t + 1, j)), [R(su, 2 * o, 2 * o + 2 * n)], [], 300.0, "left", NENG)
        else:
            cp(V("oya", o, o + n), D["p2"])
            act(V("oyi", o, o + n), D["nIn"], ACT.Identity, bias=1.0, scale=-1.0)
            act(V("oyg", o, o + n), D["Gn"], ACT.Identity, bias=0.5, scale=0.5)
            for m, (src, dst) in enumerate((("oya", "ya"), ("oyb", "yb"), ("oyi", "yi"), ("oyg", "yg"))):
                add("s", (lambda src=src, dst=dst: g.sync.dma_start(T[dst][:, o:o + n], T[src][:, o:o + n])), [R(src, o, o + n)], [], 200.0, "out%d" % (4 * j + m), 16)

    def kcalc(t):
        phase("kc", 0)
        b = 8 * (t % 2)
        kb = "p%d" % (2 + (t * NCH + NCH - 1) % 2)
        mm([(V(kb, 500, 501), [(M128("FK"), V("kacc", b + j, b + j + 1)) for j in range(NCH)])])
        ts(V("kcol", 0, 1), V(kb, 500, 501), 16384.0, ALU.add)
        ts(M128("HK"), M128("H1"), V("kcol", 0, 1), ALU.mult)

    pre(0, 0)
    for t in range(READS):
        for j in range(NCH):
            if t == 0 and j + 1 < NCH:
                pre(0, j + 1)
            s1(t, j)
            if t and j + 1 < NCH:
                pre(t, j + 1)
            choice(t, j)
            if j == NCH - 1 and t < READS - 1 and NCH > 1:
                scat(t, 0, OFF[j])
            upd(t, j)
            if j == NCH - 1:
                if t < READS - 1:
                    scat(t, OFF[j], CH[j])
                    pre(t + 1, 0)
            vote(t, j)
            post(t, j)
        if t < READS - 1:
            kcalc(t)

    order, fin = schedule(ops, EST, BONUS)
    N = len(ops)

    eng = {"v": g.vector, "t": g.tensor, "a": g.scalar, "g": g, "s": g.sync, "s2": g.scalar}
    own = {"v": "qv", "t": "qt", "a": "qa", "g": "qg"}
    phys = {"s2": "a"}
    total = {}
    clk = {q: {} for q in ("v", "t", "a", "g", "s")}
    val = [None] * N
    opclk = [None] * N
    for k in order:
        o = ops[k]
        q = phys.get(o["q"], o["q"])
        if q == "n":
            val[k] = (o["sem"], o["inc"])
            opclk[k] = {o["sem"]: o["inc"]}
            total[o["sem"]] = o["inc"]
            continue
        c = clk[q]
        ds = [d for d, w in o["deps"].items() if w and ops[d]["sem"] != "left"]
        ds.sort(key=lambda d: -fin[d])
        for d in ds:
            s, v = val[d]
            if c.get(s, 0) < v:
                eng[q].wait_ge(T.sem[s], v)
                for s2, v2 in opclk[d].items():
                    if c.get(s2, 0) < v2:
                        c[s2] = v2
        ins = o["fn"]()
        s = o["sem"] or own[q]
        total[s] = total.get(s, 0) + o["inc"]
        if s != "left":
            ins.then_inc(T.sem[s], o["inc"])
        val[k] = (s, o.get("need", total[s]))
        opclk[k] = dict(c)
        if s != "left":
            opclk[k][s] = val[k][1]
    for s in sorted(total):
        g.wait_ge(T.sem[s], total[s])
